import numpy as np
import ml_dtypes


def mxq(x, axis, fmt="e4m3"):
    dtype, down = {"e4m3": (ml_dtypes.float8_e4m3fn, 7), "e5m2": (ml_dtypes.float8_e5m2, 14)}[fmt]
    v = np.moveaxis(np.asarray(x, np.float32).astype(ml_dtypes.bfloat16).astype(np.float64), axis, -1)
    blocks = v.reshape(v.shape[:-1] + (-1, 32))
    amax = np.abs(blocks).max(-1, keepdims=True)
    byte = np.maximum(np.where(amax > 0, np.frexp(amax)[1] - 1 + 127, 0) - down, 1)
    scale = np.exp2(byte - 127.0)
    codes = (blocks / scale).astype(np.float32).astype(dtype).astype(np.float64)
    return np.moveaxis((codes * scale).reshape(v.shape), -1, axis)


WIDE = False


def mx_kscale(k):
    if not WIDE:
        return np.ones(k)
    levels = np.array([10, -10, 5, -5, 0])
    if k % 512:
        return np.exp2(np.random.permutation(np.resize(levels, k // 32))).repeat(32)
    a = np.empty((k // 512, 16))
    for p in range(k // 512):
        a[p, :8] = np.random.permutation(np.resize(levels, 8))
        for g in range(8):
            far = levels[np.abs(levels - a[p, g]) >= 10]
            a[p, g + 8] = far[np.random.randint(len(far))]
    return np.exp2(a.ravel()).repeat(32)


def f64(x):
    return np.asarray(x).astype(np.float64)


def striped(idx):
    return np.tile(idx.reshape(-1, 16).T, (8, 1)).astype(np.uint16)


def unstriped(offs):
    return offs[:16].T.reshape(-1).astype(np.int64)


K, T, E, C, N = 2048, 1280, 6, 128, 128


def by_expert(wq, xq):
    return np.concatenate([wq[e].T @ xq[:, e * C:(e + 1) * C] for e in range(E)], axis=1)


def setup_inputs():
    n = np.random.standard_normal
    s = mx_kscale(K)[:, None]
    return {
        "xT": (n((K, T)) * s).astype(np.float32),
        "w": (n((E + 1, K, N)) / np.sqrt(K) / s[None]).astype(np.float32),
        "gate": np.tile(np.random.uniform(0.2, 1.0, E * C), (N, 1)).astype(np.float32),
        "offs": striped(np.random.permutation(T)[:E * C]),
    }


def reference(xT, w, gate, offs):
    idx = unstriped(offs)
    wq = mxq(f64(w), 1, "e4m3")
    xs = mxq(f64(xT), 0, "e4m3")
    ys = wq[E].T @ xs
    xq = mxq(f64(xT)[:, idx], 0, "e4m3")
    y = by_expert(wq, xq)
    out = ys
    out[:, idx] += f64(gate) * y
    return out

@@ -1,0 +1,256 @@
+from contextlib import ExitStack
+
+import concourse.mybir as mybir
+
+K, T, E, C, N = 2048, 1280, 6, 128, 128
+S = E * C
+
+FLOPS = 2 * K * N * (S + T)
+
+F32 = mybir.dt.float32
+BF16 = mybir.dt.bfloat16
+U32 = mybir.dt.uint32
+U16 = mybir.dt.uint16
+U8 = mybir.dt.uint8
+FP8X4 = mybir.dt.float8_e4m3fn_x4
+ADD = mybir.AluOpType.add
+MULT = mybir.AluOpType.mult
+
+P = 128
+KP = 512
+G = K // KP
+BANKS = ((0, 512), (512, 1024), (1024, 1280))
+
+
+def tile_moe_shr_lin_none_kernel(tc, xT, w, gate, offs, out):
+    nc = tc.nc
+    with ExitStack() as ctx:
+        keep = ctx.enter_context(tc.tile_pool(name="keep", bufs=1))
+        xraw_pool = ctx.enter_context(tc.tile_pool(name="xraw", bufs=3))
+        wraw_pool = ctx.enter_context(tc.tile_pool(name="wraw", bufs=3))
+        pair_pool = ctx.enter_context(tc.tile_pool(name="pairs", bufs=2))
+        gp_pool = ctx.enter_context(tc.tile_pool(name="gpp", bufs=5))
+        gq_pool = ctx.enter_context(tc.tile_pool(name="gqp", bufs=2))
+        quad_pool = ctx.enter_context(tc.tile_pool(name="quadp", bufs=2))
+        wring = ctx.enter_context(tc.tile_pool(name="wring", bufs=7))
+        psum = ctx.enter_context(tc.psum_pool(name="psum", bufs=1))
+
+        offsets = keep.tile([P, S // 16], U16, name="offsets")
+        nc.sync.dma_start(offsets[:], offs)
+
+        xc = keep.tile([P, G, T], U32, name="xc", align_bytes=64)
+        xs = keep.tile([P, G, T], U8, name="xs", align_bytes=64)
+        gc = keep.tile([P, G, S], U32, name="gc", align_bytes=64)
+        gs = keep.tile([P, G, S], U8, name="gs", align_bytes=64)
+        wc = keep.tile([P, E + 1, KP], U32, name="wc", align_bytes=64)
+        ws = keep.tile([P, E + 1, KP], U8, name="ws", align_bytes=64)
+        window = keep.tile([P, T], F32, name="window")
+        result = keep.tile([P, T], F32, name="result")
+        gates = keep.tile([P, S], F32, name="gates")
+        y = keep.tile([P, S], F32, name="y")
+        nc.gpsimd.memset(window[:], 0.0)
+
+        shared = [psum.tile([P, b - a], F32, name=f"shared{a}") for a, b in BANKS]
+        routed = [psum.tile([P, 512], F32, name="routed0"), psum.tile([P, 256], F32, name="routed1")]
+
+        raws, pairs, wraws, wquads = {}, {}, {}, {}
+
+        def load_x(g, u, cuts=(0, T)):
+            raw = xraw_pool.tile([P, 2, T], F32, name="xraw")
+            src = xT[g * KP : (g + 1) * KP, :].rearrange("(p u e) t -> p u e t", u=2, e=2)
+            for a, b in zip(cuts[:-1], cuts[1:]):
+                nc.sync.dma_start(raw[:, :, a:b], src[:, u, :, a:b])
+            raws[g, u] = raw
+
+        def load_w(e, cuts=(0, G)):
+            raw = wraw_pool.tile([P, G, KP], F32, name="wraw")
+            src = w[e].rearrange("(g p j) n -> p g (j n)", p=P, j=4)
+            for a, b in zip(cuts[:-1], cuts[1:]):
+                nc.sync.dma_start(raw[:, a:b, :], src[:, a:b, :])
+            wraws[e] = raw
+
+        def cast_x(engine_copy, g, u, a=0, b=T):
+            if g not in pairs:
+                pairs[g] = pair_pool.tile([P, 2, 2 * T], BF16, name="pairs", align_bytes=64)
+            engine_copy(
+                out=pairs[g][:, u, :].rearrange("p (t e) -> p t e", e=2)[:, a:b, :],
+                in_=raws[g, u][:, :, a:b].rearrange("p e t -> p t e"),
+            )
+
+        def cast_w(engine_copy, e, a=0, b=G):
+            if e not in wquads:
+                wquads[e] = wring.tile([P, G, KP], BF16, name="wquad", align_bytes=64)
+            if engine_copy is GP:
+                GP(
+                    wquads[e][:, a:b, :].rearrange("p g (n j) -> p g n j", j=4),
+                    wraws[e][:, a:b, :].rearrange("p g (j n) -> p g n j", j=4),
+                )
+                return
+            engine_copy(
+                out=wquads[e][:, a:b, :].rearrange("p g (c i j) -> p g c j i", i=4, j=4),
+                in_=wraws[e][:, a:b, :].rearrange("p g (j c i) -> p g c j i", i=4, j=4),
+            )
+
+        def quant_w(e, a=0, b=G):
+            nc.vector.quantize_mx(
+                out=wc[:, e, a * N : b * N].bitcast(FP8X4),
+                scales=ws[:, e, a * N : b * N],
+                in_=wquads[e][:, a:b, :].rearrange("p g c -> p (g c)"),
+            )
+
+        gp, gq, quads = {}, {}, {}
+
+        def weave(engine_copy, dst, src):
+            engine_copy(
+                out=dst.bitcast(F32).rearrange("p (t u) -> p t u", u=2),
+                in_=src.bitcast(F32).rearrange("p u t -> p t u"),
+            )
+
+        def gather(g, u):
+            if g not in gp:
+                gp[g] = gp_pool.tile([P, 2, 2 * S], BF16, name="gp", align_bytes=64)
+            nc.vector.tensor_copy(gp[g][:, u, :].bitcast(U32), pairs[g][:, u, :].bitcast(U32).indirect(offsets[:]))
+
+        def weave_tokens(engine_copy, g):
+            quads[g] = quad_pool.tile([P, 4 * T], BF16, name="quads", align_bytes=64)
+            weave(engine_copy, quads[g][:], pairs[g][:])
+
+        def weave_slots(engine_copy, g):
+            gq[g] = gq_pool.tile([P, 4 * S], BF16, name="gq", align_bytes=64)
+            weave(engine_copy, gq[g][:], gp[g][:])
+
+        def quant_tokens(g):
+            for a, b in ((0, 1024), (1024, 1280)):
+                nc.vector.quantize_mx(out=xc[:, g, a:b].bitcast(FP8X4), scales=xs[:, g, a:b], in_=quads[g][:, 4 * a : 4 * b])
+
+        def quant_slots(g):
+            for a, b in ((0, 512), (512, 768)):
+                nc.vector.quantize_mx(out=gc[:, g, a:b].bitcast(FP8X4), scales=gs[:, g, a:b], in_=gq[g][:, 4 * a : 4 * b])
+
+        def mm_shared(g):
+            for bank, (a, b) in zip(shared, BANKS):
+                nc.tensor.matmul_mx(
+                    out=bank[:],
+                    lhsT=wc[:, E, g * N : (g + 1) * N].bitcast(FP8X4),
+                    lhsT_scale=ws[:, E, g * N : (g + 1) * N],
+                    rhs=xc[:, g, a:b].bitcast(FP8X4),
+                    rhs_scale=xs[:, g, a:b],
+                    start=(g == 0),
+                    stop=(g == G - 1),
+                )
+
+        def mm_routed(e):
+            bank = routed[e // 4][:, (e % 4) * C : (e % 4 + 1) * C]
+            for g in range(G):
+                nc.tensor.matmul_mx(
+                    out=bank,
+                    lhsT=wc[:, e, g * N : (g + 1) * N].bitcast(FP8X4),
+                    lhsT_scale=ws[:, e, g * N : (g + 1) * N],
+                    rhs=gc[:, g, e * C : (e + 1) * C].bitcast(FP8X4),
+                    rhs_scale=gs[:, g, e * C : (e + 1) * C],
+                    start=(g == 0),
+                    stop=(g == G - 1),
+                )
+
+        def ycopy(engine_copy, lo, hi):
+            engine_copy(out=y[:, lo * C : hi * C], in_=routed[lo // 4][:, 0 : (hi - lo) * C])
+
+        def scatter(a, b):
+            nc.vector.tensor_tensor(
+                window[:].indirect(offsets[:, a // 16 : b // 16]), y[:, a:b], gates[:, a:b], MULT
+            )
+
+        V, A = nc.vector.tensor_copy, nc.scalar.copy
+
+        def GP(out, in_):
+            nc.gpsimd.tensor_scalar(out, in_, 1.0, 0.0, MULT, ADD)
+
+        H = T // 2
+
+        load_x(3,0)
+        load_x(3,1,(0,640,1280))
+        cast_x(A,3,1,640,896)
+        load_x(1,1,(0,512,896,1280))
+        cast_x(V,3,1,896,1280)
+        cast_x(V,3,0)
+        cast_x(A,3,1,0,384)
+        load_x(0,0)
+        cast_x(A,3,1,384,640)
+        load_x(1,0)
+        gather(3,1)
+        weave_tokens(V,3)
+        load_w(3,(0,2,4))
+        cast_x(A,1,1,0,512)
+        cast_w(GP,3,0,2)
+        cast_x(A,1,1,512,1280)
+        cast_w(GP,3,2,4)
+        cast_x(A,1,0)
+        load_x(0,1)
+        gather(3,0)
+        quant_tokens(3)
+        load_w(6,(0,2,4))
+        weave_tokens(A,1)
+        cast_x(A,0,0)
+        load_x(2,0)
+        weave_slots(V,3)
+        cast_x(V,0,1)
+        gather(1,1)
+        cast_w(A,6)
+        load_x(2,1)
+        load_w(5,(0,2,4))
+        weave_tokens(V,0)
+        gather(1,0)
+        quant_tokens(1)
+        cast_x(A,2,0)
+        cast_w(GP,5,2,4)
+        weave_slots(A,1)
+        load_w(0,(0,2,4))
+        cast_w(A,5,0,2)
+        cast_w(GP,0,0,2)
+        cast_x(A,2,1)
+        quant_tokens(0)
+        gather(0,0)
+        quant_w(6)
+        quant_slots(3)
+        cast_w(GP,0,2,4)
+        load_w(2,(0,2,4))
+        quant_w(5)
+        load_w(4)
+        load_w(1,(0,2,4))
+        weave_tokens(A,2)
+        gather(2,1)
+        quant_slots(1)
+        gather(2,0)
+        cast_w(A,4)
+        gather(0,1)
+        weave_slots(A,2)
+        quant_slots(2)
+        quant_w(0)
+        cast_w(V,1,0,2)
+        weave_slots(A,0)
+        quant_slots(0)
+        cast_w(V,2)
+        cast_w(A,1,2,4)
+        mm_routed(5)
+        mm_shared(0)
+        quant_w(2)
+        quant_w(3)
+        quant_w(4)
+        mm_routed(3)
+        mm_routed(4)
+        nc.sync.dma_start(gates[:], gate)
+        mm_routed(0)
+        ycopy(A,4,6)
+        quant_w(1)
+        mm_routed(2)
+        mm_shared(1)
+        mm_routed(1)
+        quant_tokens(2)
+        mm_shared(2)
+        ycopy(A,0,4)
+        scatter(512,768)
+        scatter(0,512)
+        mm_shared(3)
+        for bank, (a, b) in zip(shared, BANKS):
+            nc.vector.tensor_tensor(result[:, a:b], bank[:], window[:, a:b], ADD)
+            nc.sync.dma_start(out[:, a:b], result[:, a:b])

@@ -19,6 +19,8 @@ MULT = mybir.AluOpType.mult
 P = 128
 KP = 512
 G = K // KP
+H = T // 2
+COLS = T + S
 BANKS = ((0, 512), (512, 1024), (1024, 1280))
 
 
@@ -26,231 +28,154 @@ def tile_moe_shr_lin_none_kernel(tc, xT, w, gate, offs, out):
     nc = tc.nc
     with ExitStack() as ctx:
         keep = ctx.enter_context(tc.tile_pool(name="keep", bufs=1))
-        xraw_pool = ctx.enter_context(tc.tile_pool(name="xraw", bufs=3))
-        wraw_pool = ctx.enter_context(tc.tile_pool(name="wraw", bufs=3))
-        pair_pool = ctx.enter_context(tc.tile_pool(name="pairs", bufs=2))
-        gp_pool = ctx.enter_context(tc.tile_pool(name="gpp", bufs=5))
-        gq_pool = ctx.enter_context(tc.tile_pool(name="gqp", bufs=2))
-        quad_pool = ctx.enter_context(tc.tile_pool(name="quadp", bufs=2))
-        wring = ctx.enter_context(tc.tile_pool(name="wring", bufs=7))
+        raw_pool = ctx.enter_context(tc.tile_pool(name="raw", bufs=6))
         psum = ctx.enter_context(tc.psum_pool(name="psum", bufs=1))
 
-        offsets = keep.tile([P, S // 16], U16, name="offsets")
-        nc.sync.dma_start(offsets[:], offs)
+        V, A, GP = nc.vector.tensor_copy, nc.scalar.copy, nc.gpsimd.tensor_copy
 
-        xc = keep.tile([P, G, T], U32, name="xc", align_bytes=64)
-        xs = keep.tile([P, G, T], U8, name="xs", align_bytes=64)
-        gc = keep.tile([P, G, S], U32, name="gc", align_bytes=64)
-        gs = keep.tile([P, G, S], U8, name="gs", align_bytes=64)
-        wc = keep.tile([P, E + 1, KP], U32, name="wc", align_bytes=64)
-        ws = keep.tile([P, E + 1, KP], U8, name="ws", align_bytes=64)
+        offsets = keep.tile([P, S // 16], U16, name="offsets")
+        pair_tiles = [keep.tile([P, 4 * T], BF16, name=f"pairs{g}", align_bytes=64) for g in range(G)]
+        pairs = [t[:].rearrange("p (u c) -> p u c", u=2) for t in pair_tiles]
+        stage = keep.tile([P, 4 * 3072], BF16, name="stage", align_bytes=64)
+        codes = [keep.tile([P, COLS], U32, name=f"codes{g}", align_bytes=64) for g in range(G)]
+        scales = [keep.tile([P, COLS], U8, name=f"scales{g}", align_bytes=64) for g in range(G)]
+        wquads = [keep.tile([P, G * KP], BF16, name=f"wquad{e}", align_bytes=64) for e in range(E + 1)]
+        wc = [keep.tile([P, G * N], U32, name=f"wc{e}", align_bytes=64) for e in range(E + 1)]
+        ws = [keep.tile([P, G * N], U8, name=f"ws{e}", align_bytes=64) for e in range(E + 1)]
         window = keep.tile([P, T], F32, name="window")
         result = keep.tile([P, T], F32, name="result")
         gates = keep.tile([P, S], F32, name="gates")
-        y = keep.tile([P, S], F32, name="y")
         nc.gpsimd.memset(window[:], 0.0)
 
         shared = [psum.tile([P, b - a], F32, name=f"shared{a}") for a, b in BANKS]
-        routed = [psum.tile([P, 512], F32, name="routed0"), psum.tile([P, 256], F32, name="routed1")]
+        routed = [psum.tile([P, 2 * C], F32, name=f"routed{i}") for i in range(E // 2)]
 
-        raws, pairs, wraws, wquads = {}, {}, {}, {}
+        raws = {}
 
-        def load_x(g, u, cuts=(0, T)):
-            raw = xraw_pool.tile([P, 2, T], F32, name="xraw")
-            src = xT[g * KP : (g + 1) * KP, :].rearrange("(p u e) t -> p u e t", u=2, e=2)
-            for a, b in zip(cuts[:-1], cuts[1:]):
-                nc.sync.dma_start(raw[:, :, a:b], src[:, u, :, a:b])
-            raws[g, u] = raw
+        def load_x(g, u):
+            raw = raw_pool.tile([P, 2 * T], F32, name="raw")
+            dst = raw[:].rearrange("p (h e t) -> p h e t", h=2, e=2)
+            src = xT[g * KP : (g + 1) * KP, :].rearrange("(p u e) (h t) -> p u h e t", u=2, e=2, h=2)
+            for h in range(2):
+                nc.sync.dma_start(dst[:, h], src[:, u, h])
+            raws[g, u] = dst
 
-        def load_w(e, cuts=(0, G)):
-            raw = wraw_pool.tile([P, G, KP], F32, name="wraw")
+        def load_w(e, pieces):
+            raw = raw_pool.tile([P, 2 * T], F32, name="raw")
+            dst = raw[:, 0 : G * KP].rearrange("p (g c) -> p g c", g=G)
             src = w[e].rearrange("(g p j) n -> p g (j n)", p=P, j=4)
-            for a, b in zip(cuts[:-1], cuts[1:]):
-                nc.sync.dma_start(raw[:, a:b, :], src[:, a:b, :])
-            wraws[e] = raw
+            step = G // pieces
+            for a in range(0, G, step):
+                nc.sync.dma_start(dst[:, a : a + step, :], src[:, a : a + step, :])
+            raws[e] = dst
 
-        def cast_x(engine_copy, g, u, a=0, b=T):
-            if g not in pairs:
-                pairs[g] = pair_pool.tile([P, 2, 2 * T], BF16, name="pairs", align_bytes=64)
-            engine_copy(
-                out=pairs[g][:, u, :].rearrange("p (t e) -> p t e", e=2)[:, a:b, :],
-                in_=raws[g, u][:, :, a:b].rearrange("p e t -> p t e"),
+        def cast_x(copy, g, u, h):
+            copy(
+                out=pairs[g][:, u, 2 * h * H : 2 * (h + 1) * H].rearrange("p (t e) -> p t e", e=2),
+                in_=raws[g, u][:, h].rearrange("p e t -> p t e"),
             )
 
-        def cast_w(engine_copy, e, a=0, b=G):
-            if e not in wquads:
-                wquads[e] = wring.tile([P, G, KP], BF16, name="wquad", align_bytes=64)
-            if engine_copy is GP:
-                GP(
-                    wquads[e][:, a:b, :].rearrange("p g (n j) -> p g n j", j=4),
-                    wraws[e][:, a:b, :].rearrange("p g (j n) -> p g n j", j=4),
-                )
-                return
-            engine_copy(
-                out=wquads[e][:, a:b, :].rearrange("p g (c i j) -> p g c j i", i=4, j=4),
-                in_=wraws[e][:, a:b, :].rearrange("p g (j c i) -> p g c j i", i=4, j=4),
+        def cast_w(copy, e, a, b):
+            copy(
+                out=wquads[e][:, a * KP : b * KP].rearrange("p (g c i j) -> p g c j i", g=b - a, i=4, j=4),
+                in_=raws[e][:, a:b, :].rearrange("p g (j c i) -> p g c j i", i=4, j=4),
             )
 
-        def quant_w(e, a=0, b=G):
+        def quant_w(e, a, b):
             nc.vector.quantize_mx(
-                out=wc[:, e, a * N : b * N].bitcast(FP8X4),
-                scales=ws[:, e, a * N : b * N],
-                in_=wquads[e][:, a:b, :].rearrange("p g c -> p (g c)"),
+                out=wc[e][:, a * N : b * N].bitcast(FP8X4),
+                scales=ws[e][:, a * N : b * N],
+                in_=wquads[e][:, a * KP : b * KP],
             )
 
-        gp, gq, quads = {}, {}, {}
+        def stage0(g):
+            return 1024 * (g % 2)
 
-        def weave(engine_copy, dst, src):
-            engine_copy(
-                out=dst.bitcast(F32).rearrange("p (t u) -> p t u", u=2),
-                in_=src.bitcast(F32).rearrange("p u t -> p t u"),
-            )
+        def tok0(g):
+            return S * (g % 2)
+
+        def slot0(g):
+            return T * (1 - g % 2)
+
+        def gathered(g):
+            a = (0 if g % 2 else 3072 - S) * 4
+            return stage[:, a : a + 4 * S].rearrange("p (u c) -> p u c", u=2)
 
         def gather(g, u):
-            if g not in gp:
-                gp[g] = gp_pool.tile([P, 2, 2 * S], BF16, name="gp", align_bytes=64)
-            nc.vector.tensor_copy(gp[g][:, u, :].bitcast(U32), pairs[g][:, u, :].bitcast(U32).indirect(offsets[:]))
+            V(gathered(g)[:, u, :].bitcast(U32), pairs[g][:, u, :].bitcast(U32).indirect(offsets[:]))
 
-        def weave_tokens(engine_copy, g):
-            quads[g] = quad_pool.tile([P, 4 * T], BF16, name="quads", align_bytes=64)
-            weave(engine_copy, quads[g][:], pairs[g][:])
-
-        def weave_slots(engine_copy, g):
-            gq[g] = gq_pool.tile([P, 4 * S], BF16, name="gq", align_bytes=64)
-            weave(engine_copy, gq[g][:], gp[g][:])
-
-        def quant_tokens(g):
-            for a, b in ((0, 1024), (1024, 1280)):
-                nc.vector.quantize_mx(out=xc[:, g, a:b].bitcast(FP8X4), scales=xs[:, g, a:b], in_=quads[g][:, 4 * a : 4 * b])
-
-        def quant_slots(g):
-            for a, b in ((0, 512), (512, 768)):
-                nc.vector.quantize_mx(out=gc[:, g, a:b].bitcast(FP8X4), scales=gs[:, g, a:b], in_=gq[g][:, 4 * a : 4 * b])
-
-        def mm_shared(g):
-            for bank, (a, b) in zip(shared, BANKS):
-                nc.tensor.matmul_mx(
-                    out=bank[:],
-                    lhsT=wc[:, E, g * N : (g + 1) * N].bitcast(FP8X4),
-                    lhsT_scale=ws[:, E, g * N : (g + 1) * N],
-                    rhs=xc[:, g, a:b].bitcast(FP8X4),
-                    rhs_scale=xs[:, g, a:b],
-                    start=(g == 0),
-                    stop=(g == G - 1),
-                )
-
-        def mm_routed(e):
-            bank = routed[e // 4][:, (e % 4) * C : (e % 4 + 1) * C]
-            for g in range(G):
-                nc.tensor.matmul_mx(
-                    out=bank,
-                    lhsT=wc[:, e, g * N : (g + 1) * N].bitcast(FP8X4),
-                    lhsT_scale=ws[:, e, g * N : (g + 1) * N],
-                    rhs=gc[:, g, e * C : (e + 1) * C].bitcast(FP8X4),
-                    rhs_scale=gs[:, g, e * C : (e + 1) * C],
-                    start=(g == 0),
-                    stop=(g == G - 1),
-                )
-
-        def ycopy(engine_copy, lo, hi):
-            engine_copy(out=y[:, lo * C : hi * C], in_=routed[lo // 4][:, 0 : (hi - lo) * C])
-
-        def scatter(a, b):
-            nc.vector.tensor_tensor(
-                window[:].indirect(offsets[:, a // 16 : b // 16]), y[:, a:b], gates[:, a:b], MULT
+        def weave(copy, dtype, g, col, src):
+            n = src.shape[2] // 2
+            a = 4 * (stage0(g) + col)
+            copy(
+                out=stage[:, a : a + 4 * n].bitcast(dtype).rearrange("p (t u) -> p t u", u=2),
+                in_=src.bitcast(dtype).rearrange("p u t -> p t u"),
             )
 
-        V, A = nc.vector.tensor_copy, nc.scalar.copy
+        def weave_tokens(copy, dtype, g, a, b):
+            weave(copy, dtype, g, tok0(g) + a, pairs[g][:, :, 2 * a : 2 * b])
 
-        def GP(out, in_):
-            nc.gpsimd.tensor_scalar(out, in_, 1.0, 0.0, MULT, ADD)
+        def quant_x(g, half):
+            a = 1024 * half
+            s = 4 * (stage0(g) + a)
+            nc.vector.quantize_mx(
+                out=codes[g][:, a : a + 1024].bitcast(FP8X4), scales=scales[g][:, a : a + 1024], in_=stage[:, s : s + 4096]
+            )
 
-        H = T // 2
+        def mm(bank, e, g, a, b):
+            nc.tensor.matmul_mx(
+                out=bank,
+                lhsT=wc[e][:, g * N : (g + 1) * N].bitcast(FP8X4),
+                lhsT_scale=ws[e][:, g * N : (g + 1) * N],
+                rhs=codes[g][:, a:b].bitcast(FP8X4),
+                rhs_scale=scales[g][:, a:b],
+                start=(g == 0),
+                stop=(g == G - 1),
+            )
 
-        load_x(3,0)
-        load_x(3,1,(0,640,1280))
-        cast_x(A,3,1,640,896)
-        load_x(1,1,(0,512,896,1280))
-        cast_x(V,3,1,896,1280)
-        cast_x(V,3,0)
-        cast_x(A,3,1,0,384)
-        load_x(0,0)
-        cast_x(A,3,1,384,640)
-        load_x(1,0)
-        gather(3,1)
-        weave_tokens(V,3)
-        load_w(3,(0,2,4))
-        cast_x(A,1,1,0,512)
-        cast_w(GP,3,0,2)
-        cast_x(A,1,1,512,1280)
-        cast_w(GP,3,2,4)
-        cast_x(A,1,0)
-        load_x(0,1)
-        gather(3,0)
-        quant_tokens(3)
-        load_w(6,(0,2,4))
-        weave_tokens(A,1)
-        cast_x(A,0,0)
-        load_x(2,0)
-        weave_slots(V,3)
-        cast_x(V,0,1)
-        gather(1,1)
-        cast_w(A,6)
-        load_x(2,1)
-        load_w(5,(0,2,4))
-        weave_tokens(V,0)
-        gather(1,0)
-        quant_tokens(1)
-        cast_x(A,2,0)
-        cast_w(GP,5,2,4)
-        weave_slots(A,1)
-        load_w(0,(0,2,4))
-        cast_w(A,5,0,2)
-        cast_w(GP,0,0,2)
-        cast_x(A,2,1)
-        quant_tokens(0)
-        gather(0,0)
-        quant_w(6)
-        quant_slots(3)
-        cast_w(GP,0,2,4)
-        load_w(2,(0,2,4))
-        quant_w(5)
-        load_w(4)
-        load_w(1,(0,2,4))
-        weave_tokens(A,2)
-        gather(2,1)
-        quant_slots(1)
-        gather(2,0)
-        cast_w(A,4)
-        gather(0,1)
-        weave_slots(A,2)
-        quant_slots(2)
-        quant_w(0)
-        cast_w(V,1,0,2)
-        weave_slots(A,0)
-        quant_slots(0)
-        cast_w(V,2)
-        cast_w(A,1,2,4)
-        mm_routed(5)
-        mm_shared(0)
-        quant_w(2)
-        quant_w(3)
-        quant_w(4)
-        mm_routed(3)
-        mm_routed(4)
-        nc.sync.dma_start(gates[:], gate)
-        mm_routed(0)
-        ycopy(A,4,6)
-        quant_w(1)
-        mm_routed(2)
-        mm_shared(1)
-        mm_routed(1)
-        quant_tokens(2)
-        mm_shared(2)
-        ycopy(A,0,4)
-        scatter(512,768)
-        scatter(0,512)
-        mm_shared(3)
+        load_x(0, 0)
+        nc.sync.dma_start(offsets[:], offs)
+        for g in range(G):
+            for u in range(2):
+                if (g, u) != (0, 0):
+                    load_x(g, u)
+                cast_x(A, g, u, 0)
+                cast_x(V if g == 0 else A, g, u, 1)
+                gather(g, u)
+            if g == 0:
+                weave_tokens(GP, U32, g, 0, H)
+                weave_tokens(V, F32, g, H, T)
+            else:
+                weave_tokens(GP, U32, g, 0, T)
+            weave(V, F32, g, slot0(g), gathered(g))
+            quant_x(g, g % 2)
+            quant_x(g, 1 - g % 2)
+
+        def scatter(i, y):
+            A(out=y, in_=routed[i][:])
+            a, b = 2 * C * i, 2 * C * (i + 1)
+            nc.vector.tensor_tensor(window[:].indirect(offsets[:, a // 16 : b // 16]), y, gates[:, a:b], MULT)
+
+        for e in range(E):
+            load_w(e, 2)
+            if e == 1:
+                nc.sync.dma_start(gates[:], gate)
+            cast_w(A, e, 0, 2)
+            cast_w(A, e, 2, 4)
+            quant_w(e, 0, G)
+            for g in range(G):
+                mm(routed[e // 2][:, e % 2 * C : (e % 2 + 1) * C], e, g, slot0(g) + e * C, slot0(g) + (e + 1) * C)
+            if e >= 4:
+                scatter(e - 4, raws[e][:, G - 1, 0 : 2 * C])
+
+        load_w(E, G)
+        for g in range(G):
+            cast_w(A, E, g, g + 1)
+            quant_w(E, g, g + 1)
+            if g == G - 1:
+                scatter(2, raws[E][:, g, 0 : 2 * C])
+            for bank, (a, b) in zip(shared, BANKS):
+                mm(bank[:], E, g, tok0(g) + a, tok0(g) + b)
         for bank, (a, b) in zip(shared, BANKS):
             nc.vector.tensor_tensor(result[:, a:b], bank[:], window[:, a:b], ADD)
             nc.sync.dma_start(out[:, a:b], result[:, a:b])

@@ -21,6 +21,7 @@ KP = 512
 G = K // KP
 H = T // 2
 COLS = T + S
+GROUPS = ((0, 2), (2, 4), (4, 5), (5, 6))
 BANKS = ((0, 512), (512, 1024), (1024, 1280))
 
 
@@ -28,7 +29,7 @@ def tile_moe_shr_lin_none_kernel(tc, xT, w, gate, offs, out):
     nc = tc.nc
     with ExitStack() as ctx:
         keep = ctx.enter_context(tc.tile_pool(name="keep", bufs=1))
-        raw_pool = ctx.enter_context(tc.tile_pool(name="raw", bufs=6))
+        raw_pool = ctx.enter_context(tc.tile_pool(name="raw", bufs=5))
         psum = ctx.enter_context(tc.psum_pool(name="psum", bufs=1))
 
         V, A, GP = nc.vector.tensor_copy, nc.scalar.copy, nc.gpsimd.tensor_copy
@@ -48,37 +49,41 @@ def tile_moe_shr_lin_none_kernel(tc, xT, w, gate, offs, out):
         nc.gpsimd.memset(window[:], 0.0)
 
         shared = [psum.tile([P, b - a], F32, name=f"shared{a}") for a, b in BANKS]
-        routed = [psum.tile([P, 2 * C], F32, name=f"routed{i}") for i in range(E // 2)]
+        routed = [psum.tile([P, (b - a) * C], F32, name=f"routed{a}") for a, b in GROUPS]
+        last = keep.tile([P, 2 * G * KP], F32, name="last")
 
         raws = {}
 
-        def load_x(g, u):
+        def load_x(g, u, cuts):
             raw = raw_pool.tile([P, 2 * T], F32, name="raw")
-            dst = raw[:].rearrange("p (h e t) -> p h e t", h=2, e=2)
-            src = xT[g * KP : (g + 1) * KP, :].rearrange("(p u e) (h t) -> p u h e t", u=2, e=2, h=2)
-            for h in range(2):
-                nc.sync.dma_start(dst[:, h], src[:, u, h])
-            raws[g, u] = dst
+            src = xT[g * KP : (g + 1) * KP, :].rearrange("(p u e) t -> p u e t", u=2, e=2)
+            for a, b in zip(cuts[:-1], cuts[1:]):
+                raws[g, u, a] = raw[:, 2 * a : 2 * b].rearrange("p (e t) -> p e t", e=2)
+                nc.sync.dma_start(raws[g, u, a], src[:, u, :, a:b])
 
-        def load_w(e, pieces):
-            raw = raw_pool.tile([P, 2 * T], F32, name="raw")
-            dst = raw[:, 0 : G * KP].rearrange("p (g c) -> p g c", g=G)
+        def load_w(e, dst, a, b):
             src = w[e].rearrange("(g p j) n -> p g (j n)", p=P, j=4)
-            step = G // pieces
-            for a in range(0, G, step):
-                nc.sync.dma_start(dst[:, a : a + step, :], src[:, a : a + step, :])
-            raws[e] = dst
+            dst = dst.rearrange("p (g c) -> p g c", c=KP)
+            nc.sync.dma_start(dst, src[:, a:b, :])
+            raws[e, a, b] = dst
 
-        def cast_x(copy, g, u, h):
+        def load_halves(e, raw):
+            load_w(e, raw[:, 0 : 2 * KP], 0, 2)
+            load_w(e, raw[:, 2 * KP : 4 * KP], 2, 4)
+            cast_w(A, e, 0, 2)
+            cast_w(A, e, 2, 4)
+            quant_w(e, 0, G)
+
+        def cast_x(copy, g, u, piece, a, b):
             copy(
-                out=pairs[g][:, u, 2 * h * H : 2 * (h + 1) * H].rearrange("p (t e) -> p t e", e=2),
-                in_=raws[g, u][:, h].rearrange("p e t -> p t e"),
+                out=pairs[g][:, u, 2 * a : 2 * b].rearrange("p (t e) -> p t e", e=2),
+                in_=raws[g, u, piece][:, :, a - piece : b - piece].rearrange("p e t -> p t e"),
             )
 
         def cast_w(copy, e, a, b):
             copy(
                 out=wquads[e][:, a * KP : b * KP].rearrange("p (g c i j) -> p g c j i", g=b - a, i=4, j=4),
-                in_=raws[e][:, a:b, :].rearrange("p g (j c i) -> p g c j i", i=4, j=4),
+                in_=raws[e, a, b].rearrange("p g (j c i) -> p g c j i", i=4, j=4),
             )
 
         def quant_w(e, a, b):
@@ -133,49 +138,76 @@ def tile_moe_shr_lin_none_kernel(tc, xT, w, gate, offs, out):
                 stop=(g == G - 1),
             )
 
-        load_x(0, 0)
-        nc.sync.dma_start(offsets[:], offs)
+        def mm_shared(g):
+            for bank, (a, b) in zip(shared, BANKS):
+                mm(bank[:], E, g, tok0(g) + a, tok0(g) + b)
+
+        def mm_routed(e, g):
+            i = [a <= e < b for a, b in GROUPS].index(True)
+            c = (e - GROUPS[i][0]) * C
+            mm(routed[i][:, c : c + C], e, g, slot0(g) + e * C, slot0(g) + (e + 1) * C)
+
+        def scatter(y, a, b):
+            nc.vector.tensor_tensor(window[:].indirect(offsets[:, a // 16 : b // 16]), y, gates[:, a:b], MULT)
+
         for g in range(G):
             for u in range(2):
-                if (g, u) != (0, 0):
-                    load_x(g, u)
-                cast_x(A, g, u, 0)
-                cast_x(V if g == 0 else A, g, u, 1)
+                if g == 0:
+                    load_x(g, u, (0, H, 1024, T))
+                    if u == 0:
+                        nc.sync.dma_start(offsets[:], offs)
+                    cast_x(A, g, u, 0, 0, H)
+                    cast_x(V, g, u, H, H, 1024)
+                    cast_x(V, g, u, 1024, 1024, T)
+                else:
+                    cuts = (0, T) if (g, u) in ((2, 0), (2, 1), (3, 0)) else (0, H, T)
+                    load_x(g, u, cuts)
+                    for a, b in zip(cuts[:-1], cuts[1:]):
+                        cast_x(A, g, u, a, a, b)
                 gather(g, u)
             if g == 0:
-                weave_tokens(GP, U32, g, 0, H)
-                weave_tokens(V, F32, g, H, T)
+                weave_tokens(A, F32, g, 0, H)
+                weave_tokens(GP, U32, g, H, T)
+            elif g == 1:
+                weave_tokens(GP, U32, g, 0, 896)
+                weave_tokens(V, F32, g, 896, T)
             else:
                 weave_tokens(GP, U32, g, 0, T)
             weave(V, F32, g, slot0(g), gathered(g))
             quant_x(g, g % 2)
             quant_x(g, 1 - g % 2)
+            if g == 2:
+                load_halves(E, raw_pool.tile([P, 2 * T], F32, name="raw"))
+                for h in range(3):
+                    mm_shared(h)
+        mm_shared(3)
 
-        def scatter(i, y):
-            A(out=y, in_=routed[i][:])
-            a, b = 2 * C * i, 2 * C * (i + 1)
-            nc.vector.tensor_tensor(window[:].indirect(offsets[:, a // 16 : b // 16]), y, gates[:, a:b], MULT)
-
-        for e in range(E):
-            load_w(e, 2)
-            if e == 1:
+        y_late = last[:, G * KP - 2 * C : G * KP + 2 * C]
+        for e in range(E - 1):
+            raw = raw_pool.tile([P, 2 * T], F32, name="raw") if e < 4 else last
+            load_halves(e, raw)
+            if e == 2:
                 nc.sync.dma_start(gates[:], gate)
-            cast_w(A, e, 0, 2)
-            cast_w(A, e, 2, 4)
-            quant_w(e, 0, G)
             for g in range(G):
-                mm(routed[e // 2][:, e % 2 * C : (e % 2 + 1) * C], e, g, slot0(g) + e * C, slot0(g) + (e + 1) * C)
-            if e >= 4:
-                scatter(e - 4, raws[e][:, G - 1, 0 : 2 * C])
-
-        load_w(E, G)
+                mm_routed(e, g)
+            if e == 3:
+                y = raw[:, 3 * KP : 3 * KP + 2 * C]
+                A(out=y, in_=routed[0][:])
+                scatter(y, 0, 256)
+            if e == 4:
+                A(out=y_late[:, 0 : 2 * C], in_=routed[1][:])
+                scatter(y_late[:, 0:192], 256, 448)
         for g in range(G):
-            cast_w(A, E, g, g + 1)
-            quant_w(E, g, g + 1)
-            if g == G - 1:
-                scatter(2, raws[E][:, g, 0 : 2 * C])
-            for bank, (a, b) in zip(shared, BANKS):
-                mm(bank[:], E, g, tok0(g) + a, tok0(g) + b)
+            a = G * KP + (g + 1) % G * KP
+            load_w(5, last[:, a : a + KP], g, g + 1)
+            cast_w(A, 5, g, g + 1)
+            quant_w(5, g, g + 1)
+            mm_routed(5, g)
+        A(out=y_late[:, 2 * C : 3 * C], in_=routed[2][:])
+        scatter(y_late[:, 192:352], 448, 608)
+        A(out=y_late[:, 3 * C : 4 * C], in_=routed[3][:])
+        scatter(y_late[:, 352:512], 608, 768)
+
         for bank, (a, b) in zip(shared, BANKS):
             nc.vector.tensor_tensor(result[:, a:b], bank[:], window[:, a:b], ADD)
             nc.sync.dma_start(out[:, a:b], result[:, a:b])

@@ -20,7 +20,7 @@ P = 128
 KP = 512
 G = K // KP
 H = T // 2
-COLS = T + S
+Q = 256
 GROUPS = ((0, 2), (2, 4), (4, 5), (5, 6))
 BANKS = ((0, 512), (512, 1024), (1024, 1280))
 
@@ -29,7 +29,7 @@ def tile_moe_shr_lin_none_kernel(tc, xT, w, gate, offs, out):
     nc = tc.nc
     with ExitStack() as ctx:
         keep = ctx.enter_context(tc.tile_pool(name="keep", bufs=1))
-        raw_pool = ctx.enter_context(tc.tile_pool(name="raw", bufs=5))
+        raw_pool = ctx.enter_context(tc.tile_pool(name="raw", bufs=6))
         psum = ctx.enter_context(tc.psum_pool(name="psum", bufs=1))
 
         V, A, GP = nc.vector.tensor_copy, nc.scalar.copy, nc.gpsimd.tensor_copy
@@ -37,9 +37,9 @@ def tile_moe_shr_lin_none_kernel(tc, xT, w, gate, offs, out):
         offsets = keep.tile([P, S // 16], U16, name="offsets")
         pair_tiles = [keep.tile([P, 4 * T], BF16, name=f"pairs{g}", align_bytes=64) for g in range(G)]
         pairs = [t[:].rearrange("p (u c) -> p u c", u=2) for t in pair_tiles]
-        stage = keep.tile([P, 4 * 3072], BF16, name="stage", align_bytes=64)
-        codes = [keep.tile([P, COLS], U32, name=f"codes{g}", align_bytes=64) for g in range(G)]
-        scales = [keep.tile([P, COLS], U8, name=f"scales{g}", align_bytes=64) for g in range(G)]
+        stage = keep.tile([P, 4 * 2 * S], BF16, name="stage", align_bytes=64)
+        codes = [keep.tile([P, T + S], U32, name=f"codes{g}", align_bytes=64) for g in range(G)]
+        scales = [keep.tile([P, T + S], U8, name=f"scales{g}", align_bytes=64) for g in range(G)]
         wquads = [keep.tile([P, G * KP], BF16, name=f"wquad{e}", align_bytes=64) for e in range(E + 1)]
         wc = [keep.tile([P, G * N], U32, name=f"wc{e}", align_bytes=64) for e in range(E + 1)]
         ws = [keep.tile([P, G * N], U8, name=f"ws{e}", align_bytes=64) for e in range(E + 1)]
@@ -50,40 +50,33 @@ def tile_moe_shr_lin_none_kernel(tc, xT, w, gate, offs, out):
 
         shared = [psum.tile([P, b - a], F32, name=f"shared{a}") for a, b in BANKS]
         routed = [psum.tile([P, (b - a) * C], F32, name=f"routed{a}") for a, b in GROUPS]
-        last = keep.tile([P, 2 * G * KP], F32, name="last")
 
-        raws = {}
+        def new_raw():
+            return raw_pool.tile([P, 2 * T], F32, name="raw")
 
-        def load_x(g, u, cuts):
-            raw = raw_pool.tile([P, 2 * T], F32, name="raw")
+        def load_x(g, u, pieces):
+            raw = new_raw()
             src = xT[g * KP : (g + 1) * KP, :].rearrange("(p u e) t -> p u e t", u=2, e=2)
-            for a, b in zip(cuts[:-1], cuts[1:]):
-                raws[g, u, a] = raw[:, 2 * a : 2 * b].rearrange("p (e t) -> p e t", e=2)
-                nc.sync.dma_start(raws[g, u, a], src[:, u, :, a:b])
+            views = []
+            for a, b in pieces:
+                view = raw[:, 2 * a : 2 * b].rearrange("p (e t) -> p e t", e=2)
+                nc.sync.dma_start(view, src[:, u, :, a:b])
+                views.append(view)
+            return views
 
-        def load_w(e, dst, a, b):
+        def cast_x(copy, g, u, view, a, b):
+            copy(
+                out=pairs[g][:, u, 2 * a : 2 * b].rearrange("p (t e) -> p t e", e=2),
+                in_=view.rearrange("p e t -> p t e"),
+            )
+
+        def load_cast_w(e, dst, a, b):
             src = w[e].rearrange("(g p j) n -> p g (j n)", p=P, j=4)
             dst = dst.rearrange("p (g c) -> p g c", c=KP)
             nc.sync.dma_start(dst, src[:, a:b, :])
-            raws[e, a, b] = dst
-
-        def load_halves(e, raw):
-            load_w(e, raw[:, 0 : 2 * KP], 0, 2)
-            load_w(e, raw[:, 2 * KP : 4 * KP], 2, 4)
-            cast_w(A, e, 0, 2)
-            cast_w(A, e, 2, 4)
-            quant_w(e, 0, G)
-
-        def cast_x(copy, g, u, piece, a, b):
-            copy(
-                out=pairs[g][:, u, 2 * a : 2 * b].rearrange("p (t e) -> p t e", e=2),
-                in_=raws[g, u, piece][:, :, a - piece : b - piece].rearrange("p e t -> p t e"),
-            )
-
-        def cast_w(copy, e, a, b):
-            copy(
+            A(
                 out=wquads[e][:, a * KP : b * KP].rearrange("p (g c i j) -> p g c j i", g=b - a, i=4, j=4),
-                in_=raws[e, a, b].rearrange("p g (j c i) -> p g c j i", i=4, j=4),
+                in_=dst.rearrange("p g (j c i) -> p g c j i", i=4, j=4),
             )
 
         def quant_w(e, a, b):
@@ -93,38 +86,24 @@ def tile_moe_shr_lin_none_kernel(tc, xT, w, gate, offs, out):
                 in_=wquads[e][:, a * KP : b * KP],
             )
 
-        def stage0(g):
-            return 1024 * (g % 2)
-
-        def tok0(g):
-            return S * (g % 2)
-
-        def slot0(g):
-            return T * (1 - g % 2)
-
         def gathered(g):
-            a = (0 if g % 2 else 3072 - S) * 4
-            return stage[:, a : a + 4 * S].rearrange("p (u c) -> p u c", u=2)
+            a = S * (1 - g % 2)
+            return stage[:, 4 * a : 4 * (a + S)].rearrange("p (u c) -> p u c", u=2)
 
         def gather(g, u):
             V(gathered(g)[:, u, :].bitcast(U32), pairs[g][:, u, :].bitcast(U32).indirect(offsets[:]))
 
-        def weave(copy, dtype, g, col, src):
-            n = src.shape[2] // 2
-            a = 4 * (stage0(g) + col)
+        def weave(copy, dtype, col, src, a, b):
             copy(
-                out=stage[:, a : a + 4 * n].bitcast(dtype).rearrange("p (t u) -> p t u", u=2),
-                in_=src.bitcast(dtype).rearrange("p u t -> p t u"),
+                out=stage[:, 4 * col : 4 * (col + b - a)].bitcast(dtype).rearrange("p (t u) -> p t u", u=2),
+                in_=src[:, :, 2 * a : 2 * b].bitcast(dtype).rearrange("p u t -> p t u"),
             )
 
-        def weave_tokens(copy, dtype, g, a, b):
-            weave(copy, dtype, g, tok0(g) + a, pairs[g][:, :, 2 * a : 2 * b])
-
-        def quant_x(g, half):
-            a = 1024 * half
-            s = 4 * (stage0(g) + a)
+        def quant_x(g, col, a, b):
             nc.vector.quantize_mx(
-                out=codes[g][:, a : a + 1024].bitcast(FP8X4), scales=scales[g][:, a : a + 1024], in_=stage[:, s : s + 4096]
+                out=codes[g][:, a:b].bitcast(FP8X4),
+                scales=scales[g][:, a:b],
+                in_=stage[:, 4 * col : 4 * (col + b - a)],
             )
 
         def mm(bank, e, g, a, b):
@@ -140,73 +119,101 @@ def tile_moe_shr_lin_none_kernel(tc, xT, w, gate, offs, out):
 
         def mm_shared(g):
             for bank, (a, b) in zip(shared, BANKS):
-                mm(bank[:], E, g, tok0(g) + a, tok0(g) + b)
+                mm(bank[:], E, g, a, b)
 
         def mm_routed(e, g):
             i = [a <= e < b for a, b in GROUPS].index(True)
             c = (e - GROUPS[i][0]) * C
-            mm(routed[i][:, c : c + C], e, g, slot0(g) + e * C, slot0(g) + (e + 1) * C)
+            mm(routed[i][:, c : c + C], e, g, T + e * C, T + (e + 1) * C)
 
         def scatter(y, a, b):
             nc.vector.tensor_tensor(window[:].indirect(offsets[:, a // 16 : b // 16]), y, gates[:, a:b], MULT)
 
-        for g in range(G):
-            for u in range(2):
-                if g == 0:
-                    load_x(g, u, (0, H, 1024, T))
-                    if u == 0:
-                        nc.sync.dma_start(offsets[:], offs)
-                    cast_x(A, g, u, 0, 0, H)
-                    cast_x(V, g, u, H, H, 1024)
-                    cast_x(V, g, u, 1024, 1024, T)
-                else:
-                    cuts = (0, T) if (g, u) in ((2, 0), (2, 1), (3, 0)) else (0, H, T)
-                    load_x(g, u, cuts)
-                    for a, b in zip(cuts[:-1], cuts[1:]):
-                        cast_x(A, g, u, a, a, b)
-                gather(g, u)
+        def bring_plane(g, u, second):
             if g == 0:
-                weave_tokens(A, F32, g, 0, H)
-                weave_tokens(GP, U32, g, H, T)
-            elif g == 1:
-                weave_tokens(GP, U32, g, 0, 896)
-                weave_tokens(V, F32, g, 896, T)
+                pieces = ((H, T), (0, 384), (384, H))
+                views = load_x(g, u, pieces)
+                if not second:
+                    nc.sync.dma_start(offsets[:], offs)
+                for copy, view, (a, b) in zip((A, V, V), views, pieces):
+                    cast_x(copy, g, u, view, a, b)
+            elif 2 * g + second <= 4:
+                pieces = ((0, H), (H, T))
+                for view, (a, b) in zip(load_x(g, u, pieces), pieces):
+                    cast_x(A, g, u, view, a, b)
             else:
-                weave_tokens(GP, U32, g, 0, T)
-            weave(V, F32, g, slot0(g), gathered(g))
-            quant_x(g, g % 2)
-            quant_x(g, 1 - g % 2)
-            if g == 2:
-                load_halves(E, raw_pool.tile([P, 2 * T], F32, name="raw"))
-                for h in range(3):
-                    mm_shared(h)
-        mm_shared(3)
+                view = load_x(g, u, ((0, T),))[0]
+                for a, b in ((0, S), (S, T)) if second else ((0, T),):
+                    cast_x(A, g, u, view[:, :, a:b], a, b)
 
-        y_late = last[:, G * KP - 2 * C : G * KP + 2 * C]
-        for e in range(E - 1):
-            raw = raw_pool.tile([P, 2 * T], F32, name="raw") if e < 4 else last
-            load_halves(e, raw)
-            if e == 2:
-                nc.sync.dma_start(gates[:], gate)
+        for g in range(G):
+            odd = g % 2
+            home = S * odd
+            wide = (Q * odd, Q * odd + 2 * Q)
+            narrow = (2 * Q * (1 - odd), 2 * Q * (1 - odd) + Q)
+            bring_plane(g, 1 - odd, False)
+            gather(g, 1 - odd)
+            if g > 0:
+                for half in (1 - odd, odd):
+                    quant_x(g - 1, 2 * Q + Q * half, S + Q * half, S + Q * (half + 1))
+            bring_plane(g, odd, True)
+            gather(g, odd)
+            own = 2 * Q * odd
+            weave(A, F32, home + own, pairs[g], own, own + Q)
+            rest = Q * (1 - odd)
+            weave(GP, U32, home + rest, pairs[g], rest, rest + 2 * Q)
+            for a, b in (wide, narrow):
+                quant_x(g, home + a, a, b)
+            for a, b in (wide, narrow):
+                weave(V, F32, home + a, gathered(g), a, b)
+            quant_x(g, home + wide[0], T + wide[0], T + wide[1])
+            if g == G - 1:
+                weave(V, F32, 0, pairs[g], S, T)
+            quant_x(g, home + narrow[0], T + narrow[0], T + narrow[1])
+            if g < G - 1:
+                weave(GP, U32, 2 * Q, pairs[g], S, T)
+        quant_x(G - 1, 0, S, T)
+
+        def expert(e, cuts):
+            raw = new_raw()
+            for a, b in zip(cuts[:-1], cuts[1:]):
+                load_cast_w(e, raw[:, a * KP : b * KP], a, b)
+            quant_w(e, 0, G)
             for g in range(G):
                 mm_routed(e, g)
-            if e == 3:
-                y = raw[:, 3 * KP : 3 * KP + 2 * C]
-                A(out=y, in_=routed[0][:])
-                scatter(y, 0, 256)
-            if e == 4:
-                A(out=y_late[:, 0 : 2 * C], in_=routed[1][:])
-                scatter(y_late[:, 0:192], 256, 448)
+            return raw
+
+        for e in range(3):
+            expert(e, (0, 2, 4))
+        raw = new_raw()
+        load_cast_w(E, raw[:, 0 : 2 * KP], 0, 2)
+        load_cast_w(E, raw[:, 2 * KP : 3 * KP], 2, 3)
+        nc.sync.dma_start(gates[:], gate)
+        quant_w(E, 0, 2)
+        quant_w(E, 2, 3)
+        for g in range(G - 1):
+            mm_shared(g)
+        raw = expert(3, (0, 2, 4))
+        A(out=raw[:, 0 : 2 * C], in_=routed[0][:])
+        scatter(raw[:, 0 : 2 * C], 0, 256)
+        raw = expert(4, (0, 2, 3, 4))
+        y = raw[:, 3 * KP : 3 * KP + 192]
+        A(out=y, in_=routed[1][:, 0:192])
+        scatter(y, 256, 448)
+        raw = new_raw()
         for g in range(G):
-            a = G * KP + (g + 1) % G * KP
-            load_w(5, last[:, a : a + KP], g, g + 1)
-            cast_w(A, 5, g, g + 1)
+            load_cast_w(5, raw[:, g * KP : (g + 1) * KP], g, g + 1)
             quant_w(5, g, g + 1)
             mm_routed(5, g)
-        A(out=y_late[:, 2 * C : 3 * C], in_=routed[2][:])
-        scatter(y_late[:, 192:352], 448, 608)
-        A(out=y_late[:, 3 * C : 4 * C], in_=routed[3][:])
-        scatter(y_late[:, 352:512], 608, 768)
+        y = raw[:, G * KP - 192 : G * KP + C]
+        A(out=y[:, 0:64], in_=routed[1][:, 192:256])
+        A(out=y[:, 64:192], in_=routed[2][:])
+        scatter(y[:, 0:160], 448, 608)
+        load_cast_w(E, raw[:, G * KP : (G + 1) * KP], G - 1, G)
+        quant_w(E, G - 1, G)
+        mm_shared(G - 1)
+        A(out=y[:, 192:320], in_=routed[3][:])
+        scatter(y[:, 160:320], 608, 768)
 
         for bank, (a, b) in zip(shared, BANKS):
             nc.vector.tensor_tensor(result[:, a:b], bank[:], window[:, a:b], ADD)

@@ -21,6 +21,7 @@ KP = 512
 G = K // KP
 H = T // 2
 Q = 256
+COLS = T + S
 GROUPS = ((0, 2), (2, 4), (4, 5), (5, 6))
 BANKS = ((0, 512), (512, 1024), (1024, 1280))
 
@@ -37,9 +38,11 @@ def tile_moe_shr_lin_none_kernel(tc, xT, w, gate, offs, out):
         offsets = keep.tile([P, S // 16], U16, name="offsets")
         pair_tiles = [keep.tile([P, 4 * T], BF16, name=f"pairs{g}", align_bytes=64) for g in range(G)]
         pairs = [t[:].rearrange("p (u c) -> p u c", u=2) for t in pair_tiles]
-        stage = keep.tile([P, 4 * 2 * S], BF16, name="stage", align_bytes=64)
-        codes = [keep.tile([P, T + S], U32, name=f"codes{g}", align_bytes=64) for g in range(G)]
-        scales = [keep.tile([P, T + S], U8, name=f"scales{g}", align_bytes=64) for g in range(G)]
+        stage = keep.tile([P, 4 * (S + H)], BF16, name="stage", align_bytes=64)
+        gathered_tile = keep.tile([P, 4 * S], BF16, name="gathered", align_bytes=64)
+        gathered = gathered_tile[:].rearrange("p (u c) -> p u c", u=2)
+        codes = keep.tile([P, G * COLS], U32, name="codes", align_bytes=64)
+        scales = keep.tile([P, G * COLS], U8, name="scales", align_bytes=64)
         wquads = [keep.tile([P, G * KP], BF16, name=f"wquad{e}", align_bytes=64) for e in range(E + 1)]
         wc = [keep.tile([P, G * N], U32, name=f"wc{e}", align_bytes=64) for e in range(E + 1)]
         ws = [keep.tile([P, G * N], U8, name=f"ws{e}", align_bytes=64) for e in range(E + 1)]
@@ -52,7 +55,7 @@ def tile_moe_shr_lin_none_kernel(tc, xT, w, gate, offs, out):
         routed = [psum.tile([P, (b - a) * C], F32, name=f"routed{a}") for a, b in GROUPS]
 
         def new_raw():
-            return raw_pool.tile([P, 2 * T], F32, name="raw")
+            return raw_pool.tile([P, 2 * T], F32, name="raw", align_bytes=64)
 
         def load_x(g, u, pieces):
             raw = new_raw()
@@ -86,93 +89,94 @@ def tile_moe_shr_lin_none_kernel(tc, xT, w, gate, offs, out):
                 in_=wquads[e][:, a * KP : b * KP],
             )
 
-        def gathered(g):
-            a = S * (1 - g % 2)
-            return stage[:, 4 * a : 4 * (a + S)].rearrange("p (u c) -> p u c", u=2)
-
         def gather(g, u):
-            V(gathered(g)[:, u, :].bitcast(U32), pairs[g][:, u, :].bitcast(U32).indirect(offsets[:]))
+            V(gathered[:, u, :].bitcast(U32), pairs[g][:, u, :].bitcast(U32).indirect(offsets[:]))
 
-        def weave(copy, dtype, col, src, a, b):
+        def staged(col, n):
+            return stage[:, 4 * col : 4 * (col + n)]
+
+        def weave(copy, dtype, dst, src, a, b):
             copy(
-                out=stage[:, 4 * col : 4 * (col + b - a)].bitcast(dtype).rearrange("p (t u) -> p t u", u=2),
+                out=dst.bitcast(dtype).rearrange("p (t u) -> p t u", u=2),
                 in_=src[:, :, 2 * a : 2 * b].bitcast(dtype).rearrange("p u t -> p t u"),
             )
 
-        def quant_x(g, col, a, b):
-            nc.vector.quantize_mx(
-                out=codes[g][:, a:b].bitcast(FP8X4),
-                scales=scales[g][:, a:b],
-                in_=stage[:, 4 * col : 4 * (col + b - a)],
-            )
+        def quant_x(src, a):
+            n = src.shape[1] // 4
+            nc.vector.quantize_mx(out=codes[:, a : a + n].bitcast(FP8X4), scales=scales[:, a : a + n], in_=src)
 
         def mm(bank, e, g, a, b):
             nc.tensor.matmul_mx(
                 out=bank,
                 lhsT=wc[e][:, g * N : (g + 1) * N].bitcast(FP8X4),
                 lhsT_scale=ws[e][:, g * N : (g + 1) * N],
-                rhs=codes[g][:, a:b].bitcast(FP8X4),
-                rhs_scale=scales[g][:, a:b],
+                rhs=codes[:, COLS * g + a : COLS * g + b].bitcast(FP8X4),
+                rhs_scale=scales[:, COLS * g + a : COLS * g + b],
                 start=(g == 0),
                 stop=(g == G - 1),
             )
 
         def mm_shared(g):
             for bank, (a, b) in zip(shared, BANKS):
-                mm(bank[:], E, g, a, b)
+                mm(bank[:], E, g, S + a, S + b)
 
         def mm_routed(e, g):
             i = [a <= e < b for a, b in GROUPS].index(True)
             c = (e - GROUPS[i][0]) * C
-            mm(routed[i][:, c : c + C], e, g, T + e * C, T + (e + 1) * C)
+            mm(routed[i][:, c : c + C], e, g, e * C, (e + 1) * C)
 
         def scatter(y, a, b):
             nc.vector.tensor_tensor(window[:].indirect(offsets[:, a // 16 : b // 16]), y, gates[:, a:b], MULT)
 
-        def bring_plane(g, u, second):
-            if g == 0:
-                pieces = ((H, T), (0, 384), (384, H))
-                views = load_x(g, u, pieces)
-                if not second:
-                    nc.sync.dma_start(offsets[:], offs)
-                for copy, view, (a, b) in zip((A, V, V), views, pieces):
-                    cast_x(copy, g, u, view, a, b)
-            elif 2 * g + second <= 4:
-                pieces = ((0, H), (H, T))
-                for view, (a, b) in zip(load_x(g, u, pieces), pieces):
-                    cast_x(A, g, u, view, a, b)
-            else:
-                view = load_x(g, u, ((0, T),))[0]
-                for a, b in ((0, S), (S, T)) if second else ((0, T),):
-                    cast_x(A, g, u, view[:, :, a:b], a, b)
+        def bring_plane(g, u, steps, pieces):
+            views = load_x(g, u, pieces)
+            if g == 0 and u == 0:
+                nc.sync.dma_start(offsets[:], offs)
+            for copy, a, b in steps:
+                i = [lo <= a < hi for lo, hi in pieces].index(True)
+                lo = pieces[i][0]
+                cast_x(copy, g, u, views[i][:, :, a - lo : b - lo], a, b)
+
+        halves = ((H, T), (0, H))
+        thirds = ((H, T), (0, 384), (384, H))
+        middle = ((H, T), (0, Q), (Q, H))
+        shared_casts = [(copy, a, b) for copy, (a, b) in zip((A, V, A), middle)]
+        own = [keep.tile([P, 4 * C], BF16, name=f"own{g}", align_bytes=64) for g in range(G)]
 
         for g in range(G):
-            odd = g % 2
-            home = S * odd
-            wide = (Q * odd, Q * odd + 2 * Q)
-            narrow = (2 * Q * (1 - odd), 2 * Q * (1 - odd) + Q)
-            bring_plane(g, 1 - odd, False)
-            gather(g, 1 - odd)
-            if g > 0:
-                for half in (1 - odd, odd):
-                    quant_x(g - 1, 2 * Q + Q * half, S + Q * half, S + Q * (half + 1))
-            bring_plane(g, odd, True)
-            gather(g, odd)
-            own = 2 * Q * odd
-            weave(A, F32, home + own, pairs[g], own, own + Q)
-            rest = Q * (1 - odd)
-            weave(GP, U32, home + rest, pairs[g], rest, rest + 2 * Q)
-            for a, b in (wide, narrow):
-                quant_x(g, home + a, a, b)
-            for a, b in (wide, narrow):
-                weave(V, F32, home + a, gathered(g), a, b)
-            quant_x(g, home + wide[0], T + wide[0], T + wide[1])
+            base = COLS * g
+            for u in range(2):
+                if g == 0:
+                    bring_plane(g, u, ((A, H, T), (V, 0, 384), (V, 384, H)), thirds)
+                elif g == 1 and u == 1:
+                    bring_plane(g, u, shared_casts, middle)
+                elif g > 1:
+                    bring_plane(g, u, ((A, H, T), (A, 0, H)), halves)
+                gather(g, u)
+                if g > 0 and u == 0:
+                    quant_x(staged(S, 2 * Q), base - 2 * Q)
+            weave(A, F32, own[g][:], pairs[g], H, S)
+            quant_x(own[g][:], base + S + H)
+            weave(GP, U32, staged(S, H), pairs[g], 0, H)
+            weave(V, F32, staged(0, S), gathered, 0, S)
+            if g == 0:
+                bring_plane(1, 0, shared_casts, middle)
             if g == G - 1:
-                weave(V, F32, 0, pairs[g], S, T)
-            quant_x(g, home + narrow[0], T + narrow[0], T + narrow[1])
+                raw = new_raw()
+                load_cast_w(E, raw[:, 0 : 2 * KP], 0, 2)
+                load_cast_w(E, raw[:, 2 * KP : 3 * KP], 2, 3)
+                last = raw[:, 2 * KP : 4 * KP].bitcast(BF16)
+                weave(A, F32, last, pairs[g], S, T)
+                quant_w(E, 0, 2)
+                quant_w(E, 2, 3)
+                for h in range(G - 1):
+                    mm_shared(h)
+            quant_x(staged(4 * Q, Q), base + 4 * Q)
+            quant_x(staged(5 * Q, C), base + 5 * Q)
+            quant_x(staged(0, 4 * Q), base)
             if g < G - 1:
-                weave(GP, U32, 2 * Q, pairs[g], S, T)
-        quant_x(G - 1, 0, S, T)
+                weave(GP, U32, staged(S, 2 * Q), pairs[g], S, T)
+        quant_x(last, COLS * G - 2 * Q)
 
         def expert(e, cuts):
             raw = new_raw()
@@ -185,26 +189,21 @@ def tile_moe_shr_lin_none_kernel(tc, xT, w, gate, offs, out):
 
         for e in range(3):
             expert(e, (0, 2, 4))
-        raw = new_raw()
-        load_cast_w(E, raw[:, 0 : 2 * KP], 0, 2)
-        load_cast_w(E, raw[:, 2 * KP : 3 * KP], 2, 3)
         nc.sync.dma_start(gates[:], gate)
-        quant_w(E, 0, 2)
-        quant_w(E, 2, 3)
-        for g in range(G - 1):
-            mm_shared(g)
         raw = expert(3, (0, 2, 4))
-        A(out=raw[:, 0 : 2 * C], in_=routed[0][:])
-        scatter(raw[:, 0 : 2 * C], 0, 256)
-        raw = expert(4, (0, 2, 3, 4))
-        y = raw[:, 3 * KP : 3 * KP + 192]
+        y = raw[:, 2 * KP : 2 * KP + 2 * C]
+        A(out=y, in_=routed[0][:])
+        scatter(y, 0, 256)
+        raw = expert(4, (0, 2, 4))
+        y = raw[:, 2 * KP : 2 * KP + 192]
         A(out=y, in_=routed[1][:, 0:192])
         scatter(y, 256, 448)
         raw = new_raw()
-        for g in range(G):
-            load_cast_w(5, raw[:, g * KP : (g + 1) * KP], g, g + 1)
-            quant_w(5, g, g + 1)
-            mm_routed(5, g)
+        for a, b in ((0, 2), (2, 3), (3, 4)):
+            load_cast_w(5, raw[:, a * KP : b * KP], a, b)
+            quant_w(5, a, b)
+            for g in range(a, b):
+                mm_routed(5, g)
         y = raw[:, G * KP - 192 : G * KP + C]
         A(out=y[:, 0:64], in_=routed[1][:, 192:256])
         A(out=y[:, 64:192], in_=routed[2][:])

@@ -69,8 +69,8 @@ def tile_moe_shr_lin_none_kernel(tc, xT, w, gate, offs, out):
 
         def cast_x(copy, g, u, view, a, b):
             copy(
-                out=pairs[g][:, u, 2 * a : 2 * b].rearrange("p (t e) -> p t e", e=2),
-                in_=view.rearrange("p e t -> p t e"),
+                out=pairs[g][:, u, 2 * a : 2 * b].rearrange("p (c i e) -> p c e i", i=4, e=2),
+                in_=view.rearrange("p e (c i) -> p c e i", i=4),
             )
 
         def load_cast_w(e, dst, a, b):
@@ -95,10 +95,11 @@ def tile_moe_shr_lin_none_kernel(tc, xT, w, gate, offs, out):
         def staged(col, n):
             return stage[:, 4 * col : 4 * (col + n)]
 
-        def weave(copy, dtype, dst, src, a, b):
+        def weave(copy, dtype, dst, src, a, b, n_run=False):
+            i = 2 if n_run else 1
             copy(
-                out=dst.bitcast(dtype).rearrange("p (t u) -> p t u", u=2),
-                in_=src[:, :, 2 * a : 2 * b].bitcast(dtype).rearrange("p u t -> p t u"),
+                out=dst.bitcast(dtype).rearrange("p (c i u) -> p c u i", i=i, u=2),
+                in_=src[:, :, 2 * a : 2 * b].bitcast(dtype).rearrange("p u (c i) -> p c u i", i=i),
             )
 
         def quant_x(src, a):
@@ -158,7 +159,7 @@ def tile_moe_shr_lin_none_kernel(tc, xT, w, gate, offs, out):
             weave(A, F32, own[g][:], pairs[g], H, S)
             quant_x(own[g][:], base + S + H)
             weave(GP, U32, staged(S, H), pairs[g], 0, H)
-            weave(V, F32, staged(0, S), gathered, 0, S)
+            weave(V, F32, staged(0, S), gathered, 0, S, True)
             if g == 0:
                 bring_plane(1, 0, shared_casts, middle)
             if g == G - 1:

@@ -20,32 +20,41 @@ P = 128
 KP = 512
 G = K // KP
 H = T // 2
-Q = 256
-COLS = T + S
-GROUPS = ((0, 2), (2, 4), (4, 5), (5, 6))
+LOWER, UPPER = (0, H), (H, T)
+HEAD_LOWER, HEAD_UPPER = 416, 960
 BANKS = ((0, 512), (512, 1024), (1024, 1280))
+GROUPS = ((0, 2), (2, 4), (4, 5), (5, 6))
+SCATTERS = ((0, 256), (256, 448), (448, 608), (608, 768))
+PLANE = 8 * T
 
 
 def tile_moe_shr_lin_none_kernel(tc, xT, w, gate, offs, out):
     nc = tc.nc
     with ExitStack() as ctx:
         keep = ctx.enter_context(tc.tile_pool(name="keep", bufs=1))
-        raw_pool = ctx.enter_context(tc.tile_pool(name="raw", bufs=6))
+        arena = ctx.enter_context(tc.tile_pool(name="arena", bufs=1))
         psum = ctx.enter_context(tc.psum_pool(name="psum", bufs=1))
 
         V, A, GP = nc.vector.tensor_copy, nc.scalar.copy, nc.gpsimd.tensor_copy
 
+        def place(name, cols, dtype, at):
+            return arena.tile([P, cols], dtype, name=name, offset=at, align_bytes=64)
+
+        def raw_at(g, m):
+            return (2 * g + m) * PLANE
+
+        def pairs_at(g):
+            return (2 * G + g) * PLANE
+
         offsets = keep.tile([P, S // 16], U16, name="offsets")
-        pair_tiles = [keep.tile([P, 4 * T], BF16, name=f"pairs{g}", align_bytes=64) for g in range(G)]
-        pairs = [t[:].rearrange("p (u c) -> p u c", u=2) for t in pair_tiles]
-        stage = keep.tile([P, 4 * (S + H)], BF16, name="stage", align_bytes=64)
+        stage = [keep.tile([P, 4 * S], BF16, name=f"stage{i}", align_bytes=64) for i in range(3)]
         gathered_tile = keep.tile([P, 4 * S], BF16, name="gathered", align_bytes=64)
-        gathered = gathered_tile[:].rearrange("p (u c) -> p u c", u=2)
-        codes = keep.tile([P, G * COLS], U32, name="codes", align_bytes=64)
-        scales = keep.tile([P, G * COLS], U8, name="scales", align_bytes=64)
-        wquads = [keep.tile([P, G * KP], BF16, name=f"wquad{e}", align_bytes=64) for e in range(E + 1)]
+        gathered = gathered_tile[:].rearrange("p (m c) -> p m c", m=2)
+        slot_scales = keep.tile([P, G * S], U8, name="slot_scales", align_bytes=64)
+        token_scales = keep.tile([P, G * T], U8, name="token_scales", align_bytes=64)
         wc = [keep.tile([P, G * N], U32, name=f"wc{e}", align_bytes=64) for e in range(E + 1)]
         ws = [keep.tile([P, G * N], U8, name=f"ws{e}", align_bytes=64) for e in range(E + 1)]
+        late = keep.tile([P, 4 * G * KP], F32, name="late", align_bytes=64)
         window = keep.tile([P, T], F32, name="window")
         result = keep.tile([P, T], F32, name="result")
         gates = keep.tile([P, S], F32, name="gates")
@@ -54,24 +63,85 @@ def tile_moe_shr_lin_none_kernel(tc, xT, w, gate, offs, out):
         shared = [psum.tile([P, b - a], F32, name=f"shared{a}") for a, b in BANKS]
         routed = [psum.tile([P, (b - a) * C], F32, name=f"routed{a}") for a, b in GROUPS]
 
-        def new_raw():
-            return raw_pool.tile([P, 2 * T], F32, name="raw", align_bytes=64)
+        pairs, slot_codes, token_codes = {}, {}, {}
 
-        def load_x(g, u, pieces):
-            raw = new_raw()
-            src = xT[g * KP : (g + 1) * KP, :].rearrange("(p u e) t -> p u e t", u=2, e=2)
-            views = []
-            for a, b in pieces:
-                view = raw[:, 2 * a : 2 * b].rearrange("p (e t) -> p e t", e=2)
-                nc.sync.dma_start(view, src[:, u, :, a:b])
-                views.append(view)
-            return views
+        def load_plane(g, m):
+            raw = place(f"raw{g}{m}", 2 * T, F32, raw_at(g, m))
+            src = xT[g * KP : (g + 1) * KP, :].rearrange("(p m e) t -> p m (e t)", m=2, e=2)[:, m, :]
+            nc.sync.dma_start(raw[:, H : 2 * T], src[:, H : 2 * T])
+            nc.sync.dma_start(raw[:, 0:H], src[:, 0:H])
+            return raw[:].rearrange("p (e t) -> p e t", e=2)
 
-        def cast_x(copy, g, u, view, a, b):
+        def cast_x(copy, g, m, raw, a, b):
             copy(
-                out=pairs[g][:, u, 2 * a : 2 * b].rearrange("p (c i e) -> p c e i", i=4, e=2),
-                in_=view.rearrange("p e (c i) -> p c e i", i=4),
+                out=pairs[g][:, m, 2 * a : 2 * b].rearrange("p (c i e) -> p c e i", i=4, e=2),
+                in_=raw[:, :, a:b].rearrange("p e (c i) -> p c e i", i=4),
             )
+
+        def bring_plane(g, m):
+            raw = load_plane(g, m)
+            if g == 0 and m == 1:
+                nc.sync.dma_start(offsets[:], offs)
+            if g == 0:
+                cast_x(V, g, m, raw, H, HEAD_UPPER)
+                cast_x(A, g, m, raw, HEAD_UPPER, T)
+                cast_x(V, g, m, raw, 0, HEAD_LOWER)
+                cast_x(A, g, m, raw, HEAD_LOWER, H)
+            else:
+                cast_x(A, g, m, raw, *UPPER)
+                cast_x(A, g, m, raw, *LOWER)
+
+        def gather(g, m):
+            V(gathered[:, m, :].bitcast(U32), pairs[g][:, m, :].bitcast(U32).indirect(offsets[:]))
+
+        def weave(copy, dtype, run, dst, src, a, b):
+            copy(
+                out=dst[:, 0 : 4 * (b - a)].bitcast(dtype).rearrange("p (c i m) -> p c m i", i=run, m=2),
+                in_=src[:, :, 2 * a : 2 * b].bitcast(dtype).rearrange("p m (c i) -> p c m i", i=run),
+            )
+
+        def quantize(codes, scales, src, cuts):
+            for a, b in zip(cuts[:-1], cuts[1:]):
+                nc.vector.quantize_mx(
+                    out=codes[:, a:b].bitcast(FP8X4), scales=scales[:, a:b], in_=src[:, 4 * a : 4 * b]
+                )
+
+        def quant_slots(g, src):
+            quantize(slot_codes[g], slot_scales[:, g * S : (g + 1) * S], src, (0, S // 2, S))
+
+        def quant_tokens(g, src, a, b):
+            quantize(token_codes[g][:, a:b], token_scales[:, g * T + a : g * T + b], src, (0, 384, H))
+
+        for g in range(G):
+            first, second, third = (stage[(g + i) % 3] for i in range(3))
+            pair_tile = place(f"pairs{g}", 4 * T, BF16, pairs_at(g))
+            pairs[g] = pair_tile[:].rearrange("p (m c) -> p m c", m=2)
+            bring_plane(g, 1)
+            gather(g, 1)
+            if g > 0:
+                slot_codes[g - 1] = place(f"slot_codes{g - 1}", S, U32, raw_at(g, 1))
+                quant_slots(g - 1, second)
+            bring_plane(g, 0)
+            token_codes[g] = place(f"token_codes{g}", T, U32, raw_at(g, 0))
+            early, later = (LOWER, UPPER) if g == 1 else (UPPER, LOWER)
+            if g == 0:
+                weave(A, F32, 1, first, pairs[g], *early)
+            elif g > 1:
+                weave(GP, U32, 1, first, pairs[g], *early)
+            gather(g, 0)
+            weave(GP, U32, 1, second, pairs[g], *later)
+            if g == 1:
+                weave(V, F32, 2, first, pairs[g], *early)
+                weave(V, F32, 2, third, gathered, 0, S)
+                quant_tokens(g, first, *early)
+            else:
+                quant_tokens(g, first, *early)
+                weave(V, F32, 2, third, gathered, 0, S)
+            quant_tokens(g, second, *later)
+        slot_codes[G - 1] = keep.tile([P, S], U32, name="last_slot_codes", align_bytes=64)
+        quant_slots(G - 1, stage[(G + 1) % 3])
+
+        wquads = [place(f"wquad{e}", G * KP, BF16, (e + (e > 0)) * PLANE + PLANE // 2) for e in range(E + 1)]
 
         def load_cast_w(e, dst, a, b):
             src = w[e].rearrange("(g p j) n -> p g (j n)", p=P, j=4)
@@ -83,137 +153,73 @@ def tile_moe_shr_lin_none_kernel(tc, xT, w, gate, offs, out):
             )
 
         def quant_w(e, a, b):
-            nc.vector.quantize_mx(
-                out=wc[e][:, a * N : b * N].bitcast(FP8X4),
-                scales=ws[e][:, a * N : b * N],
-                in_=wquads[e][:, a * KP : b * KP],
-            )
+            quantize(wc[e], ws[e], wquads[e], (a * N, b * N))
 
-        def gather(g, u):
-            V(gathered[:, u, :].bitcast(U32), pairs[g][:, u, :].bitcast(U32).indirect(offsets[:]))
-
-        def staged(col, n):
-            return stage[:, 4 * col : 4 * (col + n)]
-
-        def weave(copy, dtype, dst, src, a, b, n_run=False):
-            i = 2 if n_run else 1
-            copy(
-                out=dst.bitcast(dtype).rearrange("p (c i u) -> p c u i", i=i, u=2),
-                in_=src[:, :, 2 * a : 2 * b].bitcast(dtype).rearrange("p u (c i) -> p c u i", i=i),
-            )
-
-        def quant_x(src, a):
-            n = src.shape[1] // 4
-            nc.vector.quantize_mx(out=codes[:, a : a + n].bitcast(FP8X4), scales=scales[:, a : a + n], in_=src)
-
-        def mm(bank, e, g, a, b):
+        def mm(bank, e, g, codes, scales):
             nc.tensor.matmul_mx(
                 out=bank,
                 lhsT=wc[e][:, g * N : (g + 1) * N].bitcast(FP8X4),
                 lhsT_scale=ws[e][:, g * N : (g + 1) * N],
-                rhs=codes[:, COLS * g + a : COLS * g + b].bitcast(FP8X4),
-                rhs_scale=scales[:, COLS * g + a : COLS * g + b],
+                rhs=codes.bitcast(FP8X4),
+                rhs_scale=scales,
                 start=(g == 0),
                 stop=(g == G - 1),
             )
 
         def mm_shared(g):
             for bank, (a, b) in zip(shared, BANKS):
-                mm(bank[:], E, g, S + a, S + b)
+                mm(bank[:], E, g, token_codes[g][:, a:b], token_scales[:, g * T + a : g * T + b])
 
         def mm_routed(e, g):
             i = [a <= e < b for a, b in GROUPS].index(True)
             c = (e - GROUPS[i][0]) * C
-            mm(routed[i][:, c : c + C], e, g, e * C, (e + 1) * C)
+            a, b = e * C, (e + 1) * C
+            mm(routed[i][:, c : c + C], e, g, slot_codes[g][:, a:b], slot_scales[:, g * S + a : g * S + b])
 
-        def scatter(y, a, b):
-            nc.vector.tensor_tensor(window[:].indirect(offsets[:, a // 16 : b // 16]), y, gates[:, a:b], MULT)
-
-        def bring_plane(g, u, steps, pieces):
-            views = load_x(g, u, pieces)
-            if g == 0 and u == 0:
-                nc.sync.dma_start(offsets[:], offs)
-            for copy, a, b in steps:
-                i = [lo <= a < hi for lo, hi in pieces].index(True)
-                lo = pieces[i][0]
-                cast_x(copy, g, u, views[i][:, :, a - lo : b - lo], a, b)
-
-        halves = ((H, T), (0, H))
-        thirds = ((H, T), (0, 384), (384, H))
-        middle = ((H, T), (0, Q), (Q, H))
-        shared_casts = [(copy, a, b) for copy, (a, b) in zip((A, V, A), middle)]
-        own = [keep.tile([P, 4 * C], BF16, name=f"own{g}", align_bytes=64) for g in range(G)]
-
-        for g in range(G):
-            base = COLS * g
-            for u in range(2):
-                if g == 0:
-                    bring_plane(g, u, ((A, H, T), (V, 0, 384), (V, 384, H)), thirds)
-                elif g == 1 and u == 1:
-                    bring_plane(g, u, shared_casts, middle)
-                elif g > 1:
-                    bring_plane(g, u, ((A, H, T), (A, 0, H)), halves)
-                gather(g, u)
-                if g > 0 and u == 0:
-                    quant_x(staged(S, 2 * Q), base - 2 * Q)
-            weave(A, F32, own[g][:], pairs[g], H, S)
-            quant_x(own[g][:], base + S + H)
-            weave(GP, U32, staged(S, H), pairs[g], 0, H)
-            weave(V, F32, staged(0, S), gathered, 0, S, True)
-            if g == 0:
-                bring_plane(1, 0, shared_casts, middle)
-            if g == G - 1:
-                raw = new_raw()
-                load_cast_w(E, raw[:, 0 : 2 * KP], 0, 2)
-                load_cast_w(E, raw[:, 2 * KP : 3 * KP], 2, 3)
-                last = raw[:, 2 * KP : 4 * KP].bitcast(BF16)
-                weave(A, F32, last, pairs[g], S, T)
-                quant_w(E, 0, 2)
-                quant_w(E, 2, 3)
-                for h in range(G - 1):
-                    mm_shared(h)
-            quant_x(staged(4 * Q, Q), base + 4 * Q)
-            quant_x(staged(5 * Q, C), base + 5 * Q)
-            quant_x(staged(0, 4 * Q), base)
-            if g < G - 1:
-                weave(GP, U32, staged(S, 2 * Q), pairs[g], S, T)
-        quant_x(last, COLS * G - 2 * Q)
-
-        def expert(e, cuts):
-            raw = new_raw()
-            for a, b in zip(cuts[:-1], cuts[1:]):
+        def expert(e, raw):
+            for a, b in ((0, 2), (2, 4)):
                 load_cast_w(e, raw[:, a * KP : b * KP], a, b)
             quant_w(e, 0, G)
             for g in range(G):
                 mm_routed(e, g)
-            return raw
 
-        for e in range(3):
-            expert(e, (0, 2, 4))
+        def scatter(i, y):
+            a, b = SCATTERS[i]
+            nc.vector.tensor_tensor(window[:].indirect(offsets[:, a // 16 : b // 16]), y, gates[:, a:b], MULT)
+
+        for e, at in enumerate((raw_at(0, 1), pairs_at(0), pairs_at(1))):
+            expert(e, place(f"w{e}", G * KP, F32, at))
         nc.sync.dma_start(gates[:], gate)
-        raw = expert(3, (0, 2, 4))
-        y = raw[:, 2 * KP : 2 * KP + 2 * C]
+        M = G * KP
+        expert(3, late[:, 0:M])
+        y = late[:, M - 2 * C : M]
         A(out=y, in_=routed[0][:])
-        scatter(y, 0, 256)
-        raw = expert(4, (0, 2, 4))
-        y = raw[:, 2 * KP : 2 * KP + 192]
-        A(out=y, in_=routed[1][:, 0:192])
-        scatter(y, 256, 448)
-        raw = new_raw()
+        scatter(0, y)
+        expert(4, late[:, M : 2 * M])
+        y = late[:, 2 * M - 2 * C : 2 * M + 2 * C]
+        A(out=y[:, 0 : 2 * C], in_=routed[1][:])
+        scatter(1, y[:, 0:192])
+        load_cast_w(E, late[:, 2 * M : 2 * M + 2 * KP], 0, 2)
+        quant_w(E, 0, 2)
+        mm_shared(0)
+        mm_shared(1)
+        A(out=y[:, 2 * C : 3 * C], in_=routed[2][:])
+        scatter(2, y[:, 192:352])
+        raw = late[:, 2 * M + 2 * KP : 3 * M + 2 * KP]
         for a, b in ((0, 2), (2, 3), (3, 4)):
             load_cast_w(5, raw[:, a * KP : b * KP], a, b)
             quant_w(5, a, b)
             for g in range(a, b):
                 mm_routed(5, g)
-        y = raw[:, G * KP - 192 : G * KP + C]
-        A(out=y[:, 0:64], in_=routed[1][:, 192:256])
-        A(out=y[:, 64:192], in_=routed[2][:])
-        scatter(y[:, 0:160], 448, 608)
-        load_cast_w(E, raw[:, G * KP : (G + 1) * KP], G - 1, G)
-        quant_w(E, G - 1, G)
-        mm_shared(G - 1)
-        A(out=y[:, 192:320], in_=routed[3][:])
-        scatter(y[:, 160:320], 608, 768)
+        raw = late[:, 3 * M : 4 * M]
+        load_cast_w(E, raw[:, 2 * KP : 3 * KP], 2, 3)
+        quant_w(E, 2, 3)
+        mm_shared(2)
+        A(out=y[:, 3 * C : 4 * C], in_=routed[3][:])
+        scatter(3, y[:, 352:512])
+        load_cast_w(E, raw[:, 3 * KP : 4 * KP], 3, 4)
+        quant_w(E, 3, 4)
+        mm_shared(3)
 
         for bank, (a, b) in zip(shared, BANKS):
             nc.vector.tensor_tensor(result[:, a:b], bank[:], window[:, a:b], ADD)

@@ -26,6 +26,9 @@ BANKS = ((0, 512), (512, 1024), (1024, 1280))
 GROUPS = ((0, 2), (2, 4), (4, 5), (5, 6))
 SCATTERS = ((0, 256), (256, 448), (448, 608), (608, 768))
 PLANE = 8 * T
+SLOT_CUT, TOKEN_CUT = 256, 128
+SECOND_AT = H - TOKEN_CUT
+SLOTS_AT = SECOND_AT + H - SLOT_CUT
 
 
 def tile_moe_shr_lin_none_kernel(tc, xT, w, gate, offs, out):
@@ -47,7 +50,7 @@ def tile_moe_shr_lin_none_kernel(tc, xT, w, gate, offs, out):
             return (2 * G + g) * PLANE
 
         offsets = keep.tile([P, S // 16], U16, name="offsets")
-        stage = [keep.tile([P, 4 * S], BF16, name=f"stage{i}", align_bytes=64) for i in range(3)]
+        stage = [keep.tile([P, 4 * (SLOTS_AT + S)], BF16, name=f"stage{i}", align_bytes=64) for i in range(2)]
         gathered_tile = keep.tile([P, 4 * S], BF16, name="gathered", align_bytes=64)
         gathered = gathered_tile[:].rearrange("p (m c) -> p m c", m=2)
         slot_scales = keep.tile([P, G * S], U8, name="slot_scales", align_bytes=64)
@@ -107,20 +110,22 @@ def tile_moe_shr_lin_none_kernel(tc, xT, w, gate, offs, out):
                 )
 
         def quant_slots(g, src):
-            quantize(slot_codes[g], slot_scales[:, g * S : (g + 1) * S], src, (0, S // 2, S))
+            quantize(slot_codes[g], slot_scales[:, g * S : (g + 1) * S], src, (0, SLOT_CUT, S))
 
         def quant_tokens(g, src, a, b):
-            quantize(token_codes[g][:, a:b], token_scales[:, g * T + a : g * T + b], src, (0, 384, H))
+            quantize(token_codes[g][:, a:b], token_scales[:, g * T + a : g * T + b], src, (0, TOKEN_CUT, H))
 
         for g in range(G):
-            first, second, third = (stage[(g + i) % 3] for i in range(3))
+            first = stage[g % 2][:, 0 : 4 * H]
+            second = stage[(g + 1) % 2][:, 4 * SECOND_AT : 4 * (SECOND_AT + H)]
+            third = stage[g % 2][:, 4 * SLOTS_AT :]
             pair_tile = place(f"pairs{g}", 4 * T, BF16, pairs_at(g))
             pairs[g] = pair_tile[:].rearrange("p (m c) -> p m c", m=2)
             bring_plane(g, 1)
             gather(g, 1)
             if g > 0:
                 slot_codes[g - 1] = place(f"slot_codes{g - 1}", S, U32, raw_at(g, 1))
-                quant_slots(g - 1, second)
+                quant_slots(g - 1, stage[(g + 1) % 2][:, 4 * SLOTS_AT :])
             bring_plane(g, 0)
             token_codes[g] = place(f"token_codes{g}", T, U32, raw_at(g, 0))
             early, later = (LOWER, UPPER) if g == 1 else (UPPER, LOWER)
@@ -139,7 +144,7 @@ def tile_moe_shr_lin_none_kernel(tc, xT, w, gate, offs, out):
                 weave(V, F32, 2, third, gathered, 0, S)
             quant_tokens(g, second, *later)
         slot_codes[G - 1] = keep.tile([P, S], U32, name="last_slot_codes", align_bytes=64)
-        quant_slots(G - 1, stage[(G + 1) % 3])
+        quant_slots(G - 1, third)
 
         wquads = [place(f"wquad{e}", G * KP, BF16, (e + (e > 0)) * PLANE + PLANE // 2) for e in range(E + 1)]
 

@@ -26,6 +26,7 @@ BANKS = ((0, 512), (512, 1024), (1024, 1280))
 GROUPS = ((0, 2), (2, 4), (4, 5), (5, 6))
 SCATTERS = ((0, 256), (256, 448), (448, 608), (608, 768))
 PLANE = 8 * T
+WQUAD_AT = (2, 3, 4, 5, 6, 7, 0)
 SLOT_CUT, TOKEN_CUT = 256, 128
 SECOND_AT = H - TOKEN_CUT
 SLOTS_AT = SECOND_AT + H - SLOT_CUT
@@ -57,7 +58,7 @@ def tile_moe_shr_lin_none_kernel(tc, xT, w, gate, offs, out):
         token_scales = keep.tile([P, G * T], U8, name="token_scales", align_bytes=64)
         wc = [keep.tile([P, G * N], U32, name=f"wc{e}", align_bytes=64) for e in range(E + 1)]
         ws = [keep.tile([P, G * N], U8, name=f"ws{e}", align_bytes=64) for e in range(E + 1)]
-        late = keep.tile([P, 4 * G * KP], F32, name="late", align_bytes=64)
+        late = keep.tile([P, (4 * G + 1) * KP], F32, name="late", align_bytes=64)
         window = keep.tile([P, T], F32, name="window")
         result = keep.tile([P, T], F32, name="result")
         gates = keep.tile([P, S], F32, name="gates")
@@ -66,7 +67,7 @@ def tile_moe_shr_lin_none_kernel(tc, xT, w, gate, offs, out):
         shared = [psum.tile([P, b - a], F32, name=f"shared{a}") for a, b in BANKS]
         routed = [psum.tile([P, (b - a) * C], F32, name=f"routed{a}") for a, b in GROUPS]
 
-        pairs, slot_codes, token_codes = {}, {}, {}
+        pairs, slot_codes, token_codes, wquads = {}, {}, {}, {}
 
         def load_plane(g, m):
             raw = place(f"raw{g}{m}", 2 * T, F32, raw_at(g, m))
@@ -115,40 +116,9 @@ def tile_moe_shr_lin_none_kernel(tc, xT, w, gate, offs, out):
         def quant_tokens(g, src, a, b):
             quantize(token_codes[g][:, a:b], token_scales[:, g * T + a : g * T + b], src, (0, TOKEN_CUT, H))
 
-        for g in range(G):
-            first = stage[g % 2][:, 0 : 4 * H]
-            second = stage[(g + 1) % 2][:, 4 * SECOND_AT : 4 * (SECOND_AT + H)]
-            third = stage[g % 2][:, 4 * SLOTS_AT :]
-            pair_tile = place(f"pairs{g}", 4 * T, BF16, pairs_at(g))
-            pairs[g] = pair_tile[:].rearrange("p (m c) -> p m c", m=2)
-            bring_plane(g, 1)
-            gather(g, 1)
-            if g > 0:
-                slot_codes[g - 1] = place(f"slot_codes{g - 1}", S, U32, raw_at(g, 1))
-                quant_slots(g - 1, stage[(g + 1) % 2][:, 4 * SLOTS_AT :])
-            bring_plane(g, 0)
-            token_codes[g] = place(f"token_codes{g}", T, U32, raw_at(g, 0))
-            early, later = (LOWER, UPPER) if g == 1 else (UPPER, LOWER)
-            if g == 0:
-                weave(A, F32, 1, first, pairs[g], *early)
-            elif g > 1:
-                weave(GP, U32, 1, first, pairs[g], *early)
-            gather(g, 0)
-            weave(GP, U32, 1, second, pairs[g], *later)
-            if g == 1:
-                weave(V, F32, 2, first, pairs[g], *early)
-                weave(V, F32, 2, third, gathered, 0, S)
-                quant_tokens(g, first, *early)
-            else:
-                quant_tokens(g, first, *early)
-                weave(V, F32, 2, third, gathered, 0, S)
-            quant_tokens(g, second, *later)
-        slot_codes[G - 1] = keep.tile([P, S], U32, name="last_slot_codes", align_bytes=64)
-        quant_slots(G - 1, third)
-
-        wquads = [place(f"wquad{e}", G * KP, BF16, (e + (e > 0)) * PLANE + PLANE // 2) for e in range(E + 1)]
-
         def load_cast_w(e, dst, a, b):
+            if e not in wquads:
+                wquads[e] = place(f"wquad{e}", G * KP, BF16, WQUAD_AT[e] * PLANE + PLANE // 2)
             src = w[e].rearrange("(g p j) n -> p g (j n)", p=P, j=4)
             dst = dst.rearrange("p (g c) -> p g c", c=KP)
             nc.sync.dma_start(dst, src[:, a:b, :])
@@ -181,6 +151,44 @@ def tile_moe_shr_lin_none_kernel(tc, xT, w, gate, offs, out):
             a, b = e * C, (e + 1) * C
             mm(routed[i][:, c : c + C], e, g, slot_codes[g][:, a:b], slot_scales[:, g * S + a : g * S + b])
 
+        for g in range(G):
+            first = stage[g % 2][:, 0 : 4 * H]
+            second = stage[(g + 1) % 2][:, 4 * SECOND_AT : 4 * (SECOND_AT + H)]
+            third = stage[g % 2][:, 4 * SLOTS_AT :]
+            pair_tile = place(f"pairs{g}", 4 * T, BF16, pairs_at(g))
+            pairs[g] = pair_tile[:].rearrange("p (m c) -> p m c", m=2)
+            bring_plane(g, 1)
+            gather(g, 1)
+            if g > 0:
+                slot_codes[g - 1] = place(f"slot_codes{g - 1}", S, U32, raw_at(g, 1))
+                quant_slots(g - 1, stage[(g + 1) % 2][:, 4 * SLOTS_AT :])
+            bring_plane(g, 0)
+            token_codes[g] = place(f"token_codes{g}", T, U32, raw_at(g, 0))
+            early, later = (LOWER, UPPER) if g == 1 else (UPPER, LOWER)
+            if g == 0:
+                weave(A, F32, 1, first, pairs[g], *early)
+            elif g > 1:
+                weave(GP, U32, 1, first, pairs[g], *early)
+            gather(g, 0)
+            weave(GP, U32, 1, second, pairs[g], *later)
+            if g == G - 1:
+                raw = place("w_shared", (G - 1) * KP, F32, raw_at(0, 1))
+                for a, b in ((0, 2), (2, 3)):
+                    load_cast_w(E, raw[:, a * KP : b * KP], a, b)
+                    quant_w(E, a, b)
+                for h in range(G - 1):
+                    mm_shared(h)
+            if g == 1:
+                weave(V, F32, 2, first, pairs[g], *early)
+                weave(V, F32, 2, third, gathered, 0, S)
+                quant_tokens(g, first, *early)
+            else:
+                quant_tokens(g, first, *early)
+                weave(V, F32, 2, third, gathered, 0, S)
+            quant_tokens(g, second, *later)
+        slot_codes[G - 1] = keep.tile([P, S], U32, name="last_slot_codes", align_bytes=64)
+        quant_slots(G - 1, third)
+
         def expert(e, raw):
             for a, b in ((0, 2), (2, 4)):
                 load_cast_w(e, raw[:, a * KP : b * KP], a, b)
@@ -192,39 +200,33 @@ def tile_moe_shr_lin_none_kernel(tc, xT, w, gate, offs, out):
             a, b = SCATTERS[i]
             nc.vector.tensor_tensor(window[:].indirect(offsets[:, a // 16 : b // 16]), y, gates[:, a:b], MULT)
 
-        for e, at in enumerate((raw_at(0, 1), pairs_at(0), pairs_at(1))):
-            expert(e, place(f"w{e}", G * KP, F32, at))
-        nc.sync.dma_start(gates[:], gate)
         M = G * KP
-        expert(3, late[:, 0:M])
-        y = late[:, M - 2 * C : M]
+        for e in range(2):
+            expert(e, place(f"w{e}", M, F32, pairs_at(e)))
+        expert(2, late[:, 0:M])
+        nc.sync.dma_start(gates[:], gate)
+        expert(3, late[:, M : 2 * M])
+        y = late[:, 2 * M - 2 * C : 2 * M]
         A(out=y, in_=routed[0][:])
         scatter(0, y)
-        expert(4, late[:, M : 2 * M])
-        y = late[:, 2 * M - 2 * C : 2 * M + 2 * C]
+        expert(4, late[:, 2 * M : 3 * M])
+        y = late[:, 3 * M - 2 * C : 3 * M + 2 * C]
         A(out=y[:, 0 : 2 * C], in_=routed[1][:])
         scatter(1, y[:, 0:192])
-        load_cast_w(E, late[:, 2 * M : 2 * M + 2 * KP], 0, 2)
-        quant_w(E, 0, 2)
-        mm_shared(0)
-        mm_shared(1)
-        A(out=y[:, 2 * C : 3 * C], in_=routed[2][:])
-        scatter(2, y[:, 192:352])
-        raw = late[:, 2 * M + 2 * KP : 3 * M + 2 * KP]
+        raw = late[:, 3 * M : 4 * M]
         for a, b in ((0, 2), (2, 3), (3, 4)):
             load_cast_w(5, raw[:, a * KP : b * KP], a, b)
             quant_w(5, a, b)
             for g in range(a, b):
                 mm_routed(5, g)
-        raw = late[:, 3 * M : 4 * M]
-        load_cast_w(E, raw[:, 2 * KP : 3 * KP], 2, 3)
-        quant_w(E, 2, 3)
-        mm_shared(2)
+            if a == 0:
+                A(out=y[:, 2 * C : 3 * C], in_=routed[2][:])
+                scatter(2, y[:, 192:352])
+        load_cast_w(E, late[:, 4 * M : 4 * M + KP], G - 1, G)
+        quant_w(E, G - 1, G)
+        mm_shared(G - 1)
         A(out=y[:, 3 * C : 4 * C], in_=routed[3][:])
         scatter(3, y[:, 352:512])
-        load_cast_w(E, raw[:, 3 * KP : 4 * KP], 3, 4)
-        quant_w(E, 3, 4)
-        mm_shared(3)
 
         for bank, (a, b) in zip(shared, BANKS):
             nc.vector.tensor_tensor(result[:, a:b], bank[:], window[:, a:b], ADD)

@@ -26,10 +26,12 @@ BANKS = ((0, 512), (512, 1024), (1024, 1280))
 GROUPS = ((0, 2), (2, 4), (4, 5), (5, 6))
 SCATTERS = ((0, 256), (256, 448), (448, 608), (608, 768))
 PLANE = 8 * T
-WQUAD_AT = (2, 3, 4, 5, 6, 7, 0)
-SLOT_CUT, TOKEN_CUT = 256, 128
-SECOND_AT = H - TOKEN_CUT
-SLOTS_AT = SECOND_AT + H - SLOT_CUT
+PIECE = 384
+BESIDE_SECOND, MIDDLE, BESIDE_NEXT = (0, PIECE), (PIECE, T - PIECE), (T - PIECE, T)
+MIDDLE_AT = PLANE - 8 * (T - 2 * PIECE)
+PIECE_AT = PLANE - 4 * PIECE
+SLOT_CODES_AT = 2048
+WQUAD_AT = (4096, 2 * PLANE + 5120, 4 * PLANE + 5120, 6 * PLANE + 5120, PLANE + MIDDLE_AT, 3 * PLANE + MIDDLE_AT, 0)
 
 
 def tile_moe_shr_lin_none_kernel(tc, xT, w, gate, offs, out):
@@ -45,20 +47,20 @@ def tile_moe_shr_lin_none_kernel(tc, xT, w, gate, offs, out):
             return arena.tile([P, cols], dtype, name=name, offset=at, align_bytes=64)
 
         def raw_at(g, m):
-            return (2 * g + m) * PLANE
+            return (2 * g + 1 - m) * PLANE
 
         def pairs_at(g):
             return (2 * G + g) * PLANE
 
         offsets = keep.tile([P, S // 16], U16, name="offsets")
-        stage = [keep.tile([P, 4 * (SLOTS_AT + S)], BF16, name=f"stage{i}", align_bytes=64) for i in range(2)]
+        slot_stage = keep.tile([P, 4 * S], BF16, name="slot_stage", align_bytes=64)
         gathered_tile = keep.tile([P, 4 * S], BF16, name="gathered", align_bytes=64)
         gathered = gathered_tile[:].rearrange("p (m c) -> p m c", m=2)
         slot_scales = keep.tile([P, G * S], U8, name="slot_scales", align_bytes=64)
         token_scales = keep.tile([P, G * T], U8, name="token_scales", align_bytes=64)
         wc = [keep.tile([P, G * N], U32, name=f"wc{e}", align_bytes=64) for e in range(E + 1)]
         ws = [keep.tile([P, G * N], U8, name=f"ws{e}", align_bytes=64) for e in range(E + 1)]
-        late = keep.tile([P, (4 * G + 1) * KP], F32, name="late", align_bytes=64)
+        early_w = keep.tile([P, (5 * G - 1) * KP], F32, name="early_w", align_bytes=64)
         window = keep.tile([P, T], F32, name="window")
         result = keep.tile([P, T], F32, name="result")
         gates = keep.tile([P, S], F32, name="gates")
@@ -110,15 +112,15 @@ def tile_moe_shr_lin_none_kernel(tc, xT, w, gate, offs, out):
                     out=codes[:, a:b].bitcast(FP8X4), scales=scales[:, a:b], in_=src[:, 4 * a : 4 * b]
                 )
 
-        def quant_slots(g, src):
-            quantize(slot_codes[g], slot_scales[:, g * S : (g + 1) * S], src, (0, SLOT_CUT, S))
+        def quant_slots(g):
+            quantize(slot_codes[g], slot_scales[:, g * S : (g + 1) * S], slot_stage, (0, S // 2, S))
 
         def quant_tokens(g, src, a, b):
-            quantize(token_codes[g][:, a:b], token_scales[:, g * T + a : g * T + b], src, (0, TOKEN_CUT, H))
+            quantize(token_codes[g][:, a:b], token_scales[:, g * T + a : g * T + b], src, (0, b - a))
 
         def load_cast_w(e, dst, a, b):
             if e not in wquads:
-                wquads[e] = place(f"wquad{e}", G * KP, BF16, WQUAD_AT[e] * PLANE + PLANE // 2)
+                wquads[e] = place(f"wquad{e}", G * KP, BF16, WQUAD_AT[e])
             src = w[e].rearrange("(g p j) n -> p g (j n)", p=P, j=4)
             dst = dst.rearrange("p (g c) -> p g c", c=KP)
             nc.sync.dma_start(dst, src[:, a:b, :])
@@ -151,43 +153,44 @@ def tile_moe_shr_lin_none_kernel(tc, xT, w, gate, offs, out):
             a, b = e * C, (e + 1) * C
             mm(routed[i][:, c : c + C], e, g, slot_codes[g][:, a:b], slot_scales[:, g * S + a : g * S + b])
 
+        piece = keep.tile([P, 4 * PIECE], BF16, name="first_piece", align_bytes=64)
         for g in range(G):
-            first = stage[g % 2][:, 0 : 4 * H]
-            second = stage[(g + 1) % 2][:, 4 * SECOND_AT : 4 * (SECOND_AT + H)]
-            third = stage[g % 2][:, 4 * SLOTS_AT :]
             pair_tile = place(f"pairs{g}", 4 * T, BF16, pairs_at(g))
             pairs[g] = pair_tile[:].rearrange("p (m c) -> p m c", m=2)
             bring_plane(g, 1)
             gather(g, 1)
             if g > 0:
-                slot_codes[g - 1] = place(f"slot_codes{g - 1}", S, U32, raw_at(g, 1))
-                quant_slots(g - 1, stage[(g + 1) % 2][:, 4 * SLOTS_AT :])
+                piece = place(f"next{g}", 4 * PIECE, BF16, raw_at(g - 1, 0) + PIECE_AT)
+                weave(GP, U32, 1, piece, pairs[g - 1], *BESIDE_NEXT)
+                slot_codes[g - 1] = place(f"slot_codes{g - 1}", S, U32, raw_at(g, 1) + SLOT_CODES_AT)
+                quant_slots(g - 1)
+                quant_tokens(g - 1, piece, *BESIDE_NEXT)
+                piece = place(f"second{g}", 4 * PIECE, BF16, raw_at(g - 1, 0) + PIECE_AT)
             bring_plane(g, 0)
             token_codes[g] = place(f"token_codes{g}", T, U32, raw_at(g, 0))
-            early, later = (LOWER, UPPER) if g == 1 else (UPPER, LOWER)
-            if g == 0:
-                weave(A, F32, 1, first, pairs[g], *early)
-            elif g > 1:
-                weave(GP, U32, 1, first, pairs[g], *early)
             gather(g, 0)
-            weave(GP, U32, 1, second, pairs[g], *later)
-            if g == G - 1:
-                raw = place("w_shared", (G - 1) * KP, F32, raw_at(0, 1))
+            weave(GP, U32, 1, piece, pairs[g], *BESIDE_SECOND)
+            if g < G - 1:
+                middle = place(f"middle{g}", 4 * (T - 2 * PIECE), BF16, raw_at(g, 0) + MIDDLE_AT)
+                if g == 0:
+                    weave(A, F32, 1, middle, pairs[g], *MIDDLE)
+                else:
+                    weave(V, F32, 2, middle, pairs[g], *MIDDLE)
+            else:
+                middle = keep.tile([P, 4 * (T - PIECE)], BF16, name="last_tokens", align_bytes=64)
+                weave(V, F32, 2, middle, pairs[g], PIECE, T)
+                raw = early_w[:, 4 * G * KP :]
                 for a, b in ((0, 2), (2, 3)):
                     load_cast_w(E, raw[:, a * KP : b * KP], a, b)
                     quant_w(E, a, b)
                 for h in range(G - 1):
                     mm_shared(h)
-            if g == 1:
-                weave(V, F32, 2, first, pairs[g], *early)
-                weave(V, F32, 2, third, gathered, 0, S)
-                quant_tokens(g, first, *early)
-            else:
-                quant_tokens(g, first, *early)
-                weave(V, F32, 2, third, gathered, 0, S)
-            quant_tokens(g, second, *later)
+            weave(V, F32, 2, slot_stage, gathered, 0, S)
+            quant_tokens(g, piece, *BESIDE_SECOND)
+            quant_tokens(g, middle, *MIDDLE)
+        quant_tokens(G - 1, middle[:, 4 * (T - 2 * PIECE) :], *BESIDE_NEXT)
         slot_codes[G - 1] = keep.tile([P, S], U32, name="last_slot_codes", align_bytes=64)
-        quant_slots(G - 1, third)
+        quant_slots(G - 1)
 
         def expert(e, raw):
             for a, b in ((0, 2), (2, 4)):
@@ -201,28 +204,26 @@ def tile_moe_shr_lin_none_kernel(tc, xT, w, gate, offs, out):
             nc.vector.tensor_tensor(window[:].indirect(offsets[:, a // 16 : b // 16]), y, gates[:, a:b], MULT)
 
         M = G * KP
-        for e in range(2):
-            expert(e, place(f"w{e}", M, F32, pairs_at(e)))
-        expert(2, late[:, 0:M])
+        for e in range(3):
+            expert(e, early_w[:, e * M : (e + 1) * M])
         nc.sync.dma_start(gates[:], gate)
-        expert(3, late[:, M : 2 * M])
-        y = late[:, 2 * M - 2 * C : 2 * M]
+        expert(3, early_w[:, 3 * M : 4 * M])
+        y = early_w[:, 4 * M - 2 * C : 4 * M]
         A(out=y, in_=routed[0][:])
         scatter(0, y)
-        expert(4, late[:, 2 * M : 3 * M])
-        y = late[:, 3 * M - 2 * C : 3 * M + 2 * C]
+        late_w = place("late_w", 2 * M + KP, F32, pairs_at(0))
+        expert(4, late_w[:, 0:M])
+        y = late_w[:, M - 2 * C : M + 2 * C]
         A(out=y[:, 0 : 2 * C], in_=routed[1][:])
         scatter(1, y[:, 0:192])
-        raw = late[:, 3 * M : 4 * M]
-        for a, b in ((0, 2), (2, 3), (3, 4)):
-            load_cast_w(5, raw[:, a * KP : b * KP], a, b)
+        for a, b, at in ((0, 2, M + KP), (2, 3, M + 3 * KP), (3, 4, M)):
+            load_cast_w(5, late_w[:, at : at + (b - a) * KP], a, b)
             quant_w(5, a, b)
             for g in range(a, b):
                 mm_routed(5, g)
-            if a == 0:
-                A(out=y[:, 2 * C : 3 * C], in_=routed[2][:])
-                scatter(2, y[:, 192:352])
-        load_cast_w(E, late[:, 4 * M : 4 * M + KP], G - 1, G)
+        A(out=y[:, 2 * C : 3 * C], in_=routed[2][:])
+        scatter(2, y[:, 192:352])
+        load_cast_w(E, late_w[:, 2 * M :], G - 1, G)
         quant_w(E, G - 1, G)
         mm_shared(G - 1)
         A(out=y[:, 3 * C : 4 * C], in_=routed[3][:])

@@ -26,12 +26,10 @@ BANKS = ((0, 512), (512, 1024), (1024, 1280))
 GROUPS = ((0, 2), (2, 4), (4, 5), (5, 6))
 SCATTERS = ((0, 256), (256, 448), (448, 608), (608, 768))
 PLANE = 8 * T
-PIECE = 384
-BESIDE_SECOND, MIDDLE, BESIDE_NEXT = (0, PIECE), (PIECE, T - PIECE), (T - PIECE, T)
-MIDDLE_AT = PLANE - 8 * (T - 2 * PIECE)
-PIECE_AT = PLANE - 4 * PIECE
-SLOT_CODES_AT = 2048
-WQUAD_AT = (4096, 2 * PLANE + 5120, 4 * PLANE + 5120, 6 * PLANE + 5120, PLANE + MIDDLE_AT, 3 * PLANE + MIDDLE_AT, 0)
+TOKEN_CUT = 128
+UPPER_AT = H - TOKEN_CUT
+LINK = 64
+WQUAD_AT = (4096, PLANE, PLANE + 4096, 2 * PLANE, 2 * PLANE + 4096, 3 * PLANE, 0)
 
 
 def tile_moe_shr_lin_none_kernel(tc, xT, w, gate, offs, out):
@@ -47,7 +45,7 @@ def tile_moe_shr_lin_none_kernel(tc, xT, w, gate, offs, out):
             return arena.tile([P, cols], dtype, name=name, offset=at, align_bytes=64)
 
         def raw_at(g, m):
-            return (2 * g + 1 - m) * PLANE
+            return (g + G * (1 - m)) * PLANE
 
         def pairs_at(g):
             return (2 * G + g) * PLANE
@@ -116,7 +114,7 @@ def tile_moe_shr_lin_none_kernel(tc, xT, w, gate, offs, out):
             quantize(slot_codes[g], slot_scales[:, g * S : (g + 1) * S], slot_stage, (0, S // 2, S))
 
         def quant_tokens(g, src, a, b):
-            quantize(token_codes[g][:, a:b], token_scales[:, g * T + a : g * T + b], src, (0, b - a))
+            quantize(token_codes[g][:, a:b], token_scales[:, g * T + a : g * T + b], src, (0, TOKEN_CUT, H))
 
         def load_cast_w(e, dst, a, b):
             if e not in wquads:
@@ -153,44 +151,35 @@ def tile_moe_shr_lin_none_kernel(tc, xT, w, gate, offs, out):
             a, b = e * C, (e + 1) * C
             mm(routed[i][:, c : c + C], e, g, slot_codes[g][:, a:b], slot_scales[:, g * S + a : g * S + b])
 
-        piece = keep.tile([P, 4 * PIECE], BF16, name="first_piece", align_bytes=64)
         for g in range(G):
             pair_tile = place(f"pairs{g}", 4 * T, BF16, pairs_at(g))
             pairs[g] = pair_tile[:].rearrange("p (m c) -> p m c", m=2)
             bring_plane(g, 1)
             gather(g, 1)
-            if g > 0:
-                piece = place(f"next{g}", 4 * PIECE, BF16, raw_at(g - 1, 0) + PIECE_AT)
-                weave(GP, U32, 1, piece, pairs[g - 1], *BESIDE_NEXT)
-                slot_codes[g - 1] = place(f"slot_codes{g - 1}", S, U32, raw_at(g, 1) + SLOT_CODES_AT)
-                quant_slots(g - 1)
-                quant_tokens(g - 1, piece, *BESIDE_NEXT)
-                piece = place(f"second{g}", 4 * PIECE, BF16, raw_at(g - 1, 0) + PIECE_AT)
+            if g == 0:
+                woven = place("woven0", 4 * H, BF16, raw_at(0, 1) + PLANE // 2)
+            else:
+                woven = place(f"woven{g}", (PLANE + LINK) // 2, BF16, raw_at(g, 1) - LINK)
+                weave(GP, U32, 1, woven[:, 4 * UPPER_AT :], pairs[g - 1], *UPPER)
+                quant_tokens(g - 1, woven[:, 4 * UPPER_AT :], *UPPER)
             bring_plane(g, 0)
             token_codes[g] = place(f"token_codes{g}", T, U32, raw_at(g, 0))
+            slot_codes[g] = place(f"slot_codes{g}", S, U32, raw_at(g, 0) + PLANE // 2)
             gather(g, 0)
-            weave(GP, U32, 1, piece, pairs[g], *BESIDE_SECOND)
-            if g < G - 1:
-                middle = place(f"middle{g}", 4 * (T - 2 * PIECE), BF16, raw_at(g, 0) + MIDDLE_AT)
-                if g == 0:
-                    weave(A, F32, 1, middle, pairs[g], *MIDDLE)
-                else:
-                    weave(V, F32, 2, middle, pairs[g], *MIDDLE)
-            else:
-                middle = keep.tile([P, 4 * (T - PIECE)], BF16, name="last_tokens", align_bytes=64)
-                weave(V, F32, 2, middle, pairs[g], PIECE, T)
+            weave(GP, U32, 1, woven, pairs[g], *LOWER)
+            weave(V, F32, 2, slot_stage, gathered, 0, S)
+            if g == G - 1:
                 raw = early_w[:, 4 * G * KP :]
                 for a, b in ((0, 2), (2, 3)):
                     load_cast_w(E, raw[:, a * KP : b * KP], a, b)
                     quant_w(E, a, b)
                 for h in range(G - 1):
                     mm_shared(h)
-            weave(V, F32, 2, slot_stage, gathered, 0, S)
-            quant_tokens(g, piece, *BESIDE_SECOND)
-            quant_tokens(g, middle, *MIDDLE)
-        quant_tokens(G - 1, middle[:, 4 * (T - 2 * PIECE) :], *BESIDE_NEXT)
-        slot_codes[G - 1] = keep.tile([P, S], U32, name="last_slot_codes", align_bytes=64)
-        quant_slots(G - 1)
+            quant_tokens(g, woven, *LOWER)
+            if g == G - 1:
+                weave(V, F32, 2, woven[:, 4 * UPPER_AT :], pairs[g], *UPPER)
+            quant_slots(g)
+        quant_tokens(G - 1, woven[:, 4 * UPPER_AT :], *UPPER)
 
         def expert(e, raw):
             for a, b in ((0, 2), (2, 4)):

@@ -26,8 +26,9 @@ BANKS = ((0, 512), (512, 1024), (1024, 1280))
 GROUPS = ((0, 2), (2, 4), (4, 5), (5, 6))
 SCATTERS = ((0, 256), (256, 448), (448, 608), (608, 768))
 PLANE = 8 * T
-TOKEN_CUT = 128
-UPPER_AT = H - TOKEN_CUT
+CUT = 128
+UPPER_AT = H - CUT
+HEAD_PIECE = 512
 LINK = 64
 WQUAD_AT = (4096, PLANE, PLANE + 4096, 2 * PLANE, 2 * PLANE + 4096, 3 * PLANE, 0)
 
@@ -52,8 +53,9 @@ def tile_moe_shr_lin_none_kernel(tc, xT, w, gate, offs, out):
 
         offsets = keep.tile([P, S // 16], U16, name="offsets")
         slot_stage = keep.tile([P, 4 * S], BF16, name="slot_stage", align_bytes=64)
-        gathered_tile = keep.tile([P, 4 * S], BF16, name="gathered", align_bytes=64)
-        gathered = gathered_tile[:].rearrange("p (m c) -> p m c", m=2)
+        gathered_tiles = [keep.tile([P, 4 * S], BF16, name=f"gathered{i}", align_bytes=64) for i in range(2)]
+        gathered = [t[:].rearrange("p (m c) -> p m c", m=2) for t in gathered_tiles]
+        scalar_woven = keep.tile([P, 4 * (T - HEAD_PIECE)], BF16, name="scalar_woven", align_bytes=64)
         slot_scales = keep.tile([P, G * S], U8, name="slot_scales", align_bytes=64)
         token_scales = keep.tile([P, G * T], U8, name="token_scales", align_bytes=64)
         wc = [keep.tile([P, G * N], U32, name=f"wc{e}", align_bytes=64) for e in range(E + 1)]
@@ -96,7 +98,7 @@ def tile_moe_shr_lin_none_kernel(tc, xT, w, gate, offs, out):
                 cast_x(A, g, m, raw, *LOWER)
 
         def gather(g, m):
-            V(gathered[:, m, :].bitcast(U32), pairs[g][:, m, :].bitcast(U32).indirect(offsets[:]))
+            V(gathered[min(g, 1)][:, m, :].bitcast(U32), pairs[g][:, m, :].bitcast(U32).indirect(offsets[:]))
 
         def weave(copy, dtype, run, dst, src, a, b):
             copy(
@@ -110,11 +112,15 @@ def tile_moe_shr_lin_none_kernel(tc, xT, w, gate, offs, out):
                     out=codes[:, a:b].bitcast(FP8X4), scales=scales[:, a:b], in_=src[:, 4 * a : 4 * b]
                 )
 
-        def quant_slots(g):
-            quantize(slot_codes[g], slot_scales[:, g * S : (g + 1) * S], slot_stage, (0, S // 2, S))
+        def quant_slots(g, src, a, cuts):
+            quantize(slot_codes[g][:, a:S], slot_scales[:, g * S + a : (g + 1) * S], src, cuts)
 
-        def quant_tokens(g, src, a, b):
-            quantize(token_codes[g][:, a:b], token_scales[:, g * T + a : g * T + b], src, (0, TOKEN_CUT, H))
+        def quant_tokens(g, src, a, cuts):
+            quantize(token_codes[g][:, a:T], token_scales[:, g * T + a : (g + 1) * T], src, cuts)
+
+        def beside_gather(dst, src, a, b):
+            weave(GP, U32, 1, dst, src, a, a + CUT)
+            weave(GP, U32, 1, dst[:, 4 * CUT :], src, a + CUT, b)
 
         def load_cast_w(e, dst, a, b):
             if e not in wquads:
@@ -160,26 +166,37 @@ def tile_moe_shr_lin_none_kernel(tc, xT, w, gate, offs, out):
                 woven = place("woven0", 4 * H, BF16, raw_at(0, 1) + PLANE // 2)
             else:
                 woven = place(f"woven{g}", (PLANE + LINK) // 2, BF16, raw_at(g, 1) - LINK)
-                weave(GP, U32, 1, woven[:, 4 * UPPER_AT :], pairs[g - 1], *UPPER)
-                quant_tokens(g - 1, woven[:, 4 * UPPER_AT :], *UPPER)
+                if g == 1:
+                    beside_gather(woven[:, 4 * UPPER_AT :], gathered[0], CUT, S)
+                    quant_slots(0, woven[:, 4 * UPPER_AT :], CUT, (0, CUT, H))
+                else:
+                    beside_gather(woven[:, 4 * UPPER_AT :], pairs[g - 1], *UPPER)
+                    quant_tokens(g - 1, woven[:, 4 * UPPER_AT :], H, (0, CUT, H))
             bring_plane(g, 0)
             token_codes[g] = place(f"token_codes{g}", T, U32, raw_at(g, 0))
             slot_codes[g] = place(f"slot_codes{g}", S, U32, raw_at(g, 0) + PLANE // 2)
             gather(g, 0)
-            weave(GP, U32, 1, woven, pairs[g], *LOWER)
-            weave(V, F32, 2, slot_stage, gathered, 0, S)
-            if g == G - 1:
-                raw = early_w[:, 4 * G * KP :]
-                for a, b in ((0, 2), (2, 3)):
-                    load_cast_w(E, raw[:, a * KP : b * KP], a, b)
-                    quant_w(E, a, b)
-                for h in range(G - 1):
-                    mm_shared(h)
-            quant_tokens(g, woven, *LOWER)
-            if g == G - 1:
-                weave(V, F32, 2, woven[:, 4 * UPPER_AT :], pairs[g], *UPPER)
-            quant_slots(g)
-        quant_tokens(G - 1, woven[:, 4 * UPPER_AT :], *UPPER)
+            beside_gather(woven, pairs[g], 0, HEAD_PIECE if g == 0 else H)
+            quant_tokens(g, woven, 0, (0, CUT))
+            if g == 0:
+                weave(A, F32, 1, scalar_woven, pairs[g], HEAD_PIECE, T)
+                weave(V, F32, 2, slot_stage, gathered[0], 0, CUT)
+                quant_tokens(g, woven, 0, (CUT, HEAD_PIECE))
+                quant_slots(g, slot_stage, 0, (0, CUT))
+                quant_tokens(g, scalar_woven, HEAD_PIECE, (0, HEAD_PIECE, T - HEAD_PIECE))
+            else:
+                weave(V, F32, 2, slot_stage, gathered[1], 0, S)
+                if g == G - 1:
+                    weave(A, F32, 1, scalar_woven, pairs[g], *UPPER)
+                    raw = early_w[:, 4 * G * KP :]
+                    for a, b in ((0, 2), (2, 3)):
+                        load_cast_w(E, raw[:, a * KP : b * KP], a, b)
+                        quant_w(E, a, b)
+                    for h in range(G - 1):
+                        mm_shared(h)
+                quant_tokens(g, woven, 0, (CUT, H))
+                quant_slots(g, slot_stage, 0, (0, S // 2, S))
+        quant_tokens(G - 1, scalar_woven, H, (0, CUT, H))
 
         def expert(e, raw):
             for a, b in ((0, 2), (2, 4)):

@@ -26,8 +26,9 @@ BANKS = ((0, 512), (512, 1024), (1024, 1280))
 GROUPS = ((0, 2), (2, 4), (4, 5), (5, 6))
 SCATTERS = ((0, 256), (256, 448), (448, 608), (608, 768))
 PLANE = 8 * T
-CUT = 128
-UPPER_AT = H - CUT
+CUT = 256
+HEAD_SLOTS = S - H
+NEXT_AT = H - CUT
 HEAD_PIECE = 512
 LINK = 64
 WQUAD_AT = (4096, PLANE, PLANE + 4096, 2 * PLANE, 2 * PLANE + 4096, 3 * PLANE, 0)
@@ -118,9 +119,9 @@ def tile_moe_shr_lin_none_kernel(tc, xT, w, gate, offs, out):
         def quant_tokens(g, src, a, cuts):
             quantize(token_codes[g][:, a:T], token_scales[:, g * T + a : (g + 1) * T], src, cuts)
 
-        def beside_gather(dst, src, a, b):
-            weave(GP, U32, 1, dst, src, a, a + CUT)
-            weave(GP, U32, 1, dst[:, 4 * CUT :], src, a + CUT, b)
+        def beside_gather(dst, src, a, parts):
+            for lo, hi in parts:
+                weave(GP, U32, 1, dst[:, 4 * lo :], src, a + lo, a + hi)
 
         def load_cast_w(e, dst, a, b):
             if e not in wquads:
@@ -167,36 +168,38 @@ def tile_moe_shr_lin_none_kernel(tc, xT, w, gate, offs, out):
             else:
                 woven = place(f"woven{g}", (PLANE + LINK) // 2, BF16, raw_at(g, 1) - LINK)
                 if g == 1:
-                    beside_gather(woven[:, 4 * UPPER_AT :], gathered[0], CUT, S)
-                    quant_slots(0, woven[:, 4 * UPPER_AT :], CUT, (0, CUT, H))
+                    beside_gather(woven[:, 4 * NEXT_AT :], gathered[0], HEAD_SLOTS, ((0, CUT), (CUT, H)))
+                    quant_slots(0, woven[:, 4 * NEXT_AT :], HEAD_SLOTS, (0, CUT, H))
                 else:
-                    beside_gather(woven[:, 4 * UPPER_AT :], pairs[g - 1], *UPPER)
-                    quant_tokens(g - 1, woven[:, 4 * UPPER_AT :], H, (0, CUT, H))
+                    beside_gather(woven[:, 4 * NEXT_AT :], pairs[g - 1], 0, ((0, CUT), (CUT, H)))
+                    quant_tokens(g - 1, woven[:, 4 * NEXT_AT :], 0, (0, CUT, H))
             bring_plane(g, 0)
             token_codes[g] = place(f"token_codes{g}", T, U32, raw_at(g, 0))
             slot_codes[g] = place(f"slot_codes{g}", S, U32, raw_at(g, 0) + PLANE // 2)
             gather(g, 0)
-            beside_gather(woven, pairs[g], 0, HEAD_PIECE if g == 0 else H)
-            quant_tokens(g, woven, 0, (0, CUT))
             if g == 0:
+                weave(GP, U32, 1, woven, pairs[g], 0, HEAD_PIECE)
                 weave(A, F32, 1, scalar_woven, pairs[g], HEAD_PIECE, T)
-                weave(V, F32, 2, slot_stage, gathered[0], 0, CUT)
-                quant_tokens(g, woven, 0, (CUT, HEAD_PIECE))
-                quant_slots(g, slot_stage, 0, (0, CUT))
+                weave(V, F32, 2, slot_stage, gathered[0], 0, HEAD_SLOTS)
+                quant_tokens(g, woven, 0, (0, HEAD_PIECE))
+                quant_slots(g, slot_stage, 0, (0, HEAD_SLOTS))
                 quant_tokens(g, scalar_woven, HEAD_PIECE, (0, HEAD_PIECE, T - HEAD_PIECE))
             else:
+                beside_gather(woven, pairs[g], H, ((NEXT_AT, H), (0, NEXT_AT)))
+                quant_tokens(g, woven, H, (NEXT_AT, H))
                 weave(V, F32, 2, slot_stage, gathered[1], 0, S)
                 if g == G - 1:
-                    weave(A, F32, 1, scalar_woven, pairs[g], *UPPER)
                     raw = early_w[:, 4 * G * KP :]
                     for a, b in ((0, 2), (2, 3)):
                         load_cast_w(E, raw[:, a * KP : b * KP], a, b)
                         quant_w(E, a, b)
                     for h in range(G - 1):
                         mm_shared(h)
-                quant_tokens(g, woven, 0, (CUT, H))
+                quant_tokens(g, woven, H, (0, NEXT_AT))
+                if g == G - 1:
+                    weave(V, F32, 2, woven[:, 4 * NEXT_AT :], pairs[g], *LOWER)
                 quant_slots(g, slot_stage, 0, (0, S // 2, S))
-        quant_tokens(G - 1, scalar_woven, H, (0, CUT, H))
+        quant_tokens(G - 1, woven[:, 4 * NEXT_AT :], 0, (0, CUT, H))
 
         def expert(e, raw):
             for a, b in ((0, 2), (2, 4)):
@@ -222,13 +225,14 @@ def tile_moe_shr_lin_none_kernel(tc, xT, w, gate, offs, out):
         y = late_w[:, M - 2 * C : M + 2 * C]
         A(out=y[:, 0 : 2 * C], in_=routed[1][:])
         scatter(1, y[:, 0:192])
-        for a, b, at in ((0, 2, M + KP), (2, 3, M + 3 * KP), (3, 4, M)):
+        for a, b, at in ((0, 2, M + KP), (2, 3, M), (3, 4, M + 3 * KP)):
             load_cast_w(5, late_w[:, at : at + (b - a) * KP], a, b)
             quant_w(5, a, b)
             for g in range(a, b):
                 mm_routed(5, g)
-        A(out=y[:, 2 * C : 3 * C], in_=routed[2][:])
-        scatter(2, y[:, 192:352])
+            if a == 2:
+                A(out=y[:, 2 * C : 3 * C], in_=routed[2][:])
+                scatter(2, y[:, 192:352])
         load_cast_w(E, late_w[:, 2 * M :], G - 1, G)
         quant_w(E, G - 1, G)
         mm_shared(G - 1)

@@ -1,6 +1,7 @@
 from contextlib import ExitStack
 
 import concourse.mybir as mybir
+from concourse.masks import make_identity
 
 K, T, E, C, N = 2048, 1280, 6, 128, 128
 S = E * C
@@ -22,13 +23,16 @@ G = K // KP
 H = T // 2
 LOWER, UPPER = (0, H), (H, T)
 HEAD_LOWER, HEAD_UPPER = 416, 960
-BANKS = ((0, 512), (512, 1024), (1024, 1280))
+BANKS = ((0, 256), (256, 768), (768, 1280))
 GROUPS = ((0, 2), (2, 4), (4, 5), (5, 6))
 SCATTERS = ((0, 256), (256, 448), (448, 608), (608, 768))
 PLANE = 8 * T
-CUT = 256
+PIECE = 576
+CUT = PIECE - 512
+NEXT_AT = PIECE - CUT
 HEAD_SLOTS = S - H
-NEXT_AT = H - CUT
+GATE_ROWS = 8
+GATE_RUN = S // GATE_ROWS
 HEAD_PIECE = 512
 LINK = 64
 WQUAD_AT = (4096, PLANE, PLANE + 4096, 2 * PLANE, 2 * PLANE + 4096, 3 * PLANE, 0)
@@ -65,6 +69,10 @@ def tile_moe_shr_lin_none_kernel(tc, xT, w, gate, offs, out):
         window = keep.tile([P, T], F32, name="window")
         result = keep.tile([P, T], F32, name="result")
         gates = keep.tile([P, S], F32, name="gates")
+        gate_rows = keep.tile([P, P], F32, name="gate_rows")
+        identity = keep.tile([P, P], F32, name="identity")
+        nc.gpsimd.memset(gate_rows[:], 0.0)
+        make_identity(nc, identity[:])
         nc.gpsimd.memset(window[:], 0.0)
 
         shared = [psum.tile([P, b - a], F32, name=f"shared{a}") for a, b in BANKS]
@@ -89,6 +97,7 @@ def tile_moe_shr_lin_none_kernel(tc, xT, w, gate, offs, out):
             raw = load_plane(g, m)
             if g == 0 and m == 1:
                 nc.sync.dma_start(offsets[:], offs)
+                nc.sync.dma_start(gate_rows[0:GATE_ROWS, 0:GATE_RUN], gate[0, :].rearrange("(r c) -> r c", r=GATE_ROWS))
             if g == 0:
                 cast_x(V, g, m, raw, H, HEAD_UPPER)
                 cast_x(A, g, m, raw, HEAD_UPPER, T)
@@ -97,6 +106,16 @@ def tile_moe_shr_lin_none_kernel(tc, xT, w, gate, offs, out):
             else:
                 cast_x(A, g, m, raw, *UPPER)
                 cast_x(A, g, m, raw, *LOWER)
+
+        def spread_gate():
+            gate_cols = place("gate_cols", GATE_ROWS, F32, raw_at(1, 0) + PLANE // 2 + 4 * S)
+            nc.tensor.transpose(shared[0][:, 0:P], gate_rows[:], identity[:])
+            A(out=gate_cols[:], in_=shared[0][:, 0:GATE_ROWS])
+            for bank, (a, b) in zip(shared[1:], ((0, 5), (5, GATE_ROWS))):
+                for r in range(a, b):
+                    c = (r - a) * GATE_RUN
+                    nc.tensor.transpose(bank[:, c : c + P], gate_cols[:, r : r + 1].to_broadcast([P, P]), identity[:])
+                A(out=gates[:, a * GATE_RUN : b * GATE_RUN], in_=bank[:, 0 : (b - a) * GATE_RUN])
 
         def gather(g, m):
             V(gathered[min(g, 1)][:, m, :].bitcast(U32), pairs[g][:, m, :].bitcast(U32).indirect(offsets[:]))
@@ -118,10 +137,6 @@ def tile_moe_shr_lin_none_kernel(tc, xT, w, gate, offs, out):
 
         def quant_tokens(g, src, a, cuts):
             quantize(token_codes[g][:, a:T], token_scales[:, g * T + a : (g + 1) * T], src, cuts)
-
-        def beside_gather(dst, src, a, parts):
-            for lo, hi in parts:
-                weave(GP, U32, 1, dst[:, 4 * lo :], src, a + lo, a + hi)
 
         def load_cast_w(e, dst, a, b):
             if e not in wquads:
@@ -168,12 +183,14 @@ def tile_moe_shr_lin_none_kernel(tc, xT, w, gate, offs, out):
             else:
                 woven = place(f"woven{g}", (PLANE + LINK) // 2, BF16, raw_at(g, 1) - LINK)
                 if g == 1:
-                    beside_gather(woven[:, 4 * NEXT_AT :], gathered[0], HEAD_SLOTS, ((0, CUT), (CUT, H)))
-                    quant_slots(0, woven[:, 4 * NEXT_AT :], HEAD_SLOTS, (0, CUT, H))
+                    weave(GP, U32, 1, woven[:, 4 * NEXT_AT :], gathered[0], HEAD_SLOTS, S)
+                    quant_slots(0, woven[:, 4 * NEXT_AT :], HEAD_SLOTS, (0, HEAD_SLOTS, H))
                 else:
-                    beside_gather(woven[:, 4 * NEXT_AT :], pairs[g - 1], 0, ((0, CUT), (CUT, H)))
-                    quant_tokens(g - 1, woven[:, 4 * NEXT_AT :], 0, (0, CUT, H))
+                    weave(GP, U32, 1, woven[:, 4 * NEXT_AT :], pairs[g - 1], 0, PIECE)
+                    quant_tokens(g - 1, woven[:, 4 * NEXT_AT :], 0, (0, CUT, PIECE))
             bring_plane(g, 0)
+            if g == 2:
+                spread_gate()
             token_codes[g] = place(f"token_codes{g}", T, U32, raw_at(g, 0))
             slot_codes[g] = place(f"slot_codes{g}", S, U32, raw_at(g, 0) + PLANE // 2)
             gather(g, 0)
@@ -185,8 +202,10 @@ def tile_moe_shr_lin_none_kernel(tc, xT, w, gate, offs, out):
                 quant_slots(g, slot_stage, 0, (0, HEAD_SLOTS))
                 quant_tokens(g, scalar_woven, HEAD_PIECE, (0, HEAD_PIECE, T - HEAD_PIECE))
             else:
-                beside_gather(woven, pairs[g], H, ((NEXT_AT, H), (0, NEXT_AT)))
-                quant_tokens(g, woven, H, (NEXT_AT, H))
+                middle = keep.tile([P, 4 * (T - 2 * PIECE)], BF16, name=f"middle{g}", align_bytes=64)
+                weave(GP, U32, 1, woven, pairs[g], T - PIECE, T)
+                quant_tokens(g, woven, T - PIECE, (0, NEXT_AT))
+                weave(V, F32, 2, middle, pairs[g], PIECE, T - PIECE)
                 weave(V, F32, 2, slot_stage, gathered[1], 0, S)
                 if g == G - 1:
                     raw = early_w[:, 4 * G * KP :]
@@ -195,11 +214,12 @@ def tile_moe_shr_lin_none_kernel(tc, xT, w, gate, offs, out):
                         quant_w(E, a, b)
                     for h in range(G - 1):
                         mm_shared(h)
-                quant_tokens(g, woven, H, (0, NEXT_AT))
+                quant_tokens(g, woven, T - PIECE, (NEXT_AT, PIECE))
+                quant_tokens(g, middle, PIECE, (0, T - 2 * PIECE))
                 if g == G - 1:
-                    weave(V, F32, 2, woven[:, 4 * NEXT_AT :], pairs[g], *LOWER)
+                    weave(V, F32, 2, woven[:, 4 * NEXT_AT :], pairs[g], 0, PIECE)
                 quant_slots(g, slot_stage, 0, (0, S // 2, S))
-        quant_tokens(G - 1, woven[:, 4 * NEXT_AT :], 0, (0, CUT, H))
+        quant_tokens(G - 1, woven[:, 4 * NEXT_AT :], 0, (0, CUT, PIECE))
 
         def expert(e, raw):
             for a, b in ((0, 2), (2, 4)):
@@ -215,7 +235,6 @@ def tile_moe_shr_lin_none_kernel(tc, xT, w, gate, offs, out):
         M = G * KP
         for e in range(3):
             expert(e, early_w[:, e * M : (e + 1) * M])
-        nc.sync.dma_start(gates[:], gate)
         expert(3, early_w[:, 3 * M : 4 * M])
         y = early_w[:, 4 * M - 2 * C : 4 * M]
         A(out=y, in_=routed[0][:])
@@ -239,6 +258,12 @@ def tile_moe_shr_lin_none_kernel(tc, xT, w, gate, offs, out):
         A(out=y[:, 3 * C : 4 * C], in_=routed[3][:])
         scatter(3, y[:, 352:512])
 
-        for bank, (a, b) in zip(shared, BANKS):
-            nc.vector.tensor_tensor(result[:, a:b], bank[:], window[:, a:b], ADD)
-            nc.sync.dma_start(out[:, a:b], result[:, a:b])
+        a, b = BANKS[0]
+        A(out=result[:, a:b], in_=shared[0][:])
+        nc.gpsimd.tensor_tensor(result[:, a:b], result[:, a:b], window[:, a:b], ADD)
+        for i, (bank, (a, b)) in enumerate(zip(shared[1:], BANKS[1:])):
+            for lo, hi in ((a, (a + b) // 2), ((a + b) // 2, b)):
+                nc.vector.tensor_tensor(result[:, lo:hi], bank[:, lo - a : hi - a], window[:, lo:hi], ADD)
+                nc.sync.dma_start(out[:, lo:hi], result[:, lo:hi])
+            if i == 0:
+                nc.sync.dma_start(out[:, 0:a], result[:, 0:a])

@@ -47,8 +47,8 @@ def tile_moe_shr_lin_none_kernel(tc, xT, w, gate, offs, out):
 
         V, A, GP = nc.vector.tensor_copy, nc.scalar.copy, nc.gpsimd.tensor_copy
 
-        def place(name, cols, dtype, at):
-            return arena.tile([P, cols], dtype, name=name, offset=at, align_bytes=64)
+        def place(name, cols, dtype, at, align=64):
+            return arena.tile([P, cols], dtype, name=name, offset=at, align_bytes=align)
 
         def raw_at(g, m):
             return (g + G * (1 - m)) * PLANE
@@ -65,9 +65,9 @@ def tile_moe_shr_lin_none_kernel(tc, xT, w, gate, offs, out):
         token_scales = keep.tile([P, G * T], U8, name="token_scales", align_bytes=64)
         wc = [keep.tile([P, G * N], U32, name=f"wc{e}", align_bytes=64) for e in range(E + 1)]
         ws = [keep.tile([P, G * N], U8, name=f"ws{e}", align_bytes=64) for e in range(E + 1)]
-        early_w = keep.tile([P, (5 * G - 1) * KP], F32, name="early_w", align_bytes=64)
+        early_w = keep.tile([P, (5 * G - 1) * KP], F32, name="early_w", align_bytes=256)
         window = keep.tile([P, T], F32, name="window")
-        result = keep.tile([P, T], F32, name="result")
+        result = keep.tile([P, T], F32, name="result", align_bytes=256)
         gates = keep.tile([P, S], F32, name="gates")
         gate_rows = keep.tile([P, P], F32, name="gate_rows")
         identity = keep.tile([P, P], F32, name="identity")
@@ -81,7 +81,7 @@ def tile_moe_shr_lin_none_kernel(tc, xT, w, gate, offs, out):
         pairs, slot_codes, token_codes, wquads = {}, {}, {}, {}
 
         def load_plane(g, m):
-            raw = place(f"raw{g}{m}", 2 * T, F32, raw_at(g, m))
+            raw = place(f"raw{g}{m}", 2 * T, F32, raw_at(g, m), 256)
             src = xT[g * KP : (g + 1) * KP, :].rearrange("(p m e) t -> p m (e t)", m=2, e=2)[:, m, :]
             nc.sync.dma_start(raw[:, H : 2 * T], src[:, H : 2 * T])
             nc.sync.dma_start(raw[:, 0:H], src[:, 0:H])
@@ -209,17 +209,13 @@ def tile_moe_shr_lin_none_kernel(tc, xT, w, gate, offs, out):
                 weave(V, F32, 2, slot_stage, gathered[1], 0, S)
                 if g == G - 1:
                     raw = early_w[:, 4 * G * KP :]
-                    for a, b in ((0, 2), (2, 3)):
-                        load_cast_w(E, raw[:, a * KP : b * KP], a, b)
-                        quant_w(E, a, b)
-                    for h in range(G - 1):
+                    load_cast_w(E, raw[:, 0 : 2 * KP], 0, 2)
+                    quant_w(E, 0, 2)
+                    for h in range(2):
                         mm_shared(h)
                 quant_tokens(g, woven, T - PIECE, (NEXT_AT, PIECE))
                 quant_tokens(g, middle, PIECE, (0, T - 2 * PIECE))
-                if g == G - 1:
-                    weave(V, F32, 2, woven[:, 4 * NEXT_AT :], pairs[g], 0, PIECE)
                 quant_slots(g, slot_stage, 0, (0, S // 2, S))
-        quant_tokens(G - 1, woven[:, 4 * NEXT_AT :], 0, (0, CUT, PIECE))
 
         def expert(e, raw):
             for a, b in ((0, 2), (2, 4)):
@@ -233,13 +229,20 @@ def tile_moe_shr_lin_none_kernel(tc, xT, w, gate, offs, out):
             nc.vector.tensor_tensor(window[:].indirect(offsets[:, a // 16 : b // 16]), y, gates[:, a:b], MULT)
 
         M = G * KP
-        for e in range(3):
+        for e in range(2):
             expert(e, early_w[:, e * M : (e + 1) * M])
+        last = early_w[:, 2 * M - 2 * PIECE : 2 * M].bitcast(BF16)
+        weave(V, F32, 2, last, pairs[G - 1], 0, PIECE)
+        load_cast_w(E, early_w[:, 4 * M + 2 * KP :], 2, 3)
+        quant_w(E, 2, 3)
+        mm_shared(2)
+        quant_tokens(G - 1, last, 0, (0, CUT, PIECE))
+        expert(2, early_w[:, 2 * M : 3 * M])
         expert(3, early_w[:, 3 * M : 4 * M])
         y = early_w[:, 4 * M - 2 * C : 4 * M]
         A(out=y, in_=routed[0][:])
         scatter(0, y)
-        late_w = place("late_w", 2 * M + KP, F32, pairs_at(0))
+        late_w = place("late_w", 2 * M + KP, F32, pairs_at(0), 256)
         expert(4, late_w[:, 0:M])
         y = late_w[:, M - 2 * C : M + 2 * C]
         A(out=y[:, 0 : 2 * C], in_=routed[1][:])

@@ -16,6 +16,7 @@ U8 = mybir.dt.uint8
 FP8X4 = mybir.dt.float8_e4m3fn_x4
 ADD = mybir.AluOpType.add
 MULT = mybir.AluOpType.mult
+COPY = mybir.ActivationFunctionType.Copy
 
 P = 128
 KP = 512
@@ -31,10 +32,10 @@ PIECE = 576
 CUT = PIECE - 512
 NEXT_AT = PIECE - CUT
 HEAD_SLOTS = S - H
-GATE_ROWS = 8
-GATE_RUN = S // GATE_ROWS
+GATE_RUN = 3
 HEAD_PIECE = 512
 LINK = 64
+QUARTER = 4 * KP
 WQUAD_AT = (4096, PLANE, PLANE + 4096, 2 * PLANE, 2 * PLANE + 4096, 3 * PLANE, 0)
 
 
@@ -64,14 +65,12 @@ def tile_moe_shr_lin_none_kernel(tc, xT, w, gate, offs, out):
         slot_scales = keep.tile([P, G * S], U8, name="slot_scales", align_bytes=64)
         token_scales = keep.tile([P, G * T], U8, name="token_scales", align_bytes=64)
         wc = [keep.tile([P, G * N], U32, name=f"wc{e}", align_bytes=64) for e in range(E + 1)]
-        ws = [keep.tile([P, G * N], U8, name=f"ws{e}", align_bytes=64) for e in range(E + 1)]
-        early_w = keep.tile([P, (5 * G - 1) * KP], F32, name="early_w", align_bytes=256)
+        ws = {e: keep.tile([P, G * N], U8, name=f"ws{e}", align_bytes=64) for e in range(E + 1) if e != 3}
         window = keep.tile([P, T], F32, name="window")
         result = keep.tile([P, T], F32, name="result", align_bytes=256)
+        gate_cols = keep.tile([P, 2, 8], F32, name="gate_cols")
         gates = keep.tile([P, S], F32, name="gates")
-        gate_rows = keep.tile([P, P], F32, name="gate_rows")
         identity = keep.tile([P, P], F32, name="identity")
-        nc.gpsimd.memset(gate_rows[:], 0.0)
         make_identity(nc, identity[:])
         nc.gpsimd.memset(window[:], 0.0)
 
@@ -97,7 +96,6 @@ def tile_moe_shr_lin_none_kernel(tc, xT, w, gate, offs, out):
             raw = load_plane(g, m)
             if g == 0 and m == 1:
                 nc.sync.dma_start(offsets[:], offs)
-                nc.sync.dma_start(gate_rows[0:GATE_ROWS, 0:GATE_RUN], gate[0, :].rearrange("(r c) -> r c", r=GATE_ROWS))
             if g == 0:
                 cast_x(V, g, m, raw, H, HEAD_UPPER)
                 cast_x(A, g, m, raw, HEAD_UPPER, T)
@@ -108,14 +106,14 @@ def tile_moe_shr_lin_none_kernel(tc, xT, w, gate, offs, out):
                 cast_x(A, g, m, raw, *LOWER)
 
         def spread_gate():
-            gate_cols = place("gate_cols", GATE_ROWS, F32, raw_at(1, 0) + PLANE // 2 + 4 * S)
-            nc.tensor.transpose(shared[0][:, 0:P], gate_rows[:], identity[:])
-            A(out=gate_cols[:], in_=shared[0][:, 0:GATE_ROWS])
-            for bank, (a, b) in zip(shared[1:], ((0, 5), (5, GATE_ROWS))):
-                for r in range(a, b):
-                    c = (r - a) * GATE_RUN
-                    nc.tensor.transpose(bank[:, c : c + P], gate_cols[:, r : r + 1].to_broadcast([P, P]), identity[:])
-                A(out=gates[:, a * GATE_RUN : b * GATE_RUN], in_=bank[:, 0 : (b - a) * GATE_RUN])
+            nc.sync.dma_start(gate_cols[:, :, 0:GATE_RUN], gate[0, :].rearrange("(h p r) -> p h r", h=2, r=GATE_RUN))
+            for h, bank in enumerate(shared[1:]):
+                for r in range(GATE_RUN):
+                    nc.tensor.transpose(bank[:, r * P : (r + 1) * P], gate_cols[:, h, r : r + 1].to_broadcast([P, P]), identity[:])
+                V(
+                    out=gates[:, h * S // 2 : (h + 1) * S // 2].rearrange("q (p r) -> q p r", r=GATE_RUN),
+                    in_=bank[:, 0 : S // 2].rearrange("q (r p) -> q p r", r=GATE_RUN),
+                )
 
         def gather(g, m):
             V(gathered[min(g, 1)][:, m, :].bitcast(U32), pairs[g][:, m, :].bitcast(U32).indirect(offsets[:]))
@@ -138,15 +136,16 @@ def tile_moe_shr_lin_none_kernel(tc, xT, w, gate, offs, out):
         def quant_tokens(g, src, a, cuts):
             quantize(token_codes[g][:, a:T], token_scales[:, g * T + a : (g + 1) * T], src, cuts)
 
-        def load_cast_w(e, dst, a, b):
+        def load_cast_w(copy, run, e, at, a, b):
+            dst = place(f"land{e}{a}", (b - a) * KP, F32, at, 256)[:]
             if e not in wquads:
                 wquads[e] = place(f"wquad{e}", G * KP, BF16, WQUAD_AT[e])
             src = w[e].rearrange("(g p j) n -> p g (j n)", p=P, j=4)
             dst = dst.rearrange("p (g c) -> p g c", c=KP)
             nc.sync.dma_start(dst, src[:, a:b, :])
-            A(
-                out=wquads[e][:, a * KP : b * KP].rearrange("p (g c i j) -> p g c j i", g=b - a, i=4, j=4),
-                in_=dst.rearrange("p g (j c i) -> p g c j i", i=4, j=4),
+            copy(
+                out=wquads[e][:, a * KP : b * KP].rearrange("p (g c i j) -> p g c j i", g=b - a, i=run, j=4),
+                in_=dst.rearrange("p g (j c i) -> p g c j i", i=run, j=4),
             )
 
         def quant_w(e, a, b):
@@ -173,6 +172,7 @@ def tile_moe_shr_lin_none_kernel(tc, xT, w, gate, offs, out):
             a, b = e * C, (e + 1) * C
             mm(routed[i][:, c : c + C], e, g, slot_codes[g][:, a:b], slot_scales[:, g * S + a : g * S + b])
 
+        spread_gate()
         for g in range(G):
             pair_tile = place(f"pairs{g}", 4 * T, BF16, pairs_at(g))
             pairs[g] = pair_tile[:].rearrange("p (m c) -> p m c", m=2)
@@ -189,8 +189,6 @@ def tile_moe_shr_lin_none_kernel(tc, xT, w, gate, offs, out):
                     weave(GP, U32, 1, woven[:, 4 * NEXT_AT :], pairs[g - 1], 0, PIECE)
                     quant_tokens(g - 1, woven[:, 4 * NEXT_AT :], 0, (0, CUT, PIECE))
             bring_plane(g, 0)
-            if g == 2:
-                spread_gate()
             token_codes[g] = place(f"token_codes{g}", T, U32, raw_at(g, 0))
             slot_codes[g] = place(f"slot_codes{g}", S, U32, raw_at(g, 0) + PLANE // 2)
             gather(g, 0)
@@ -207,59 +205,64 @@ def tile_moe_shr_lin_none_kernel(tc, xT, w, gate, offs, out):
                 quant_tokens(g, woven, T - PIECE, (0, NEXT_AT))
                 weave(V, F32, 2, middle, pairs[g], PIECE, T - PIECE)
                 weave(V, F32, 2, slot_stage, gathered[1], 0, S)
-                if g == G - 1:
-                    raw = early_w[:, 4 * G * KP :]
-                    load_cast_w(E, raw[:, 0 : 2 * KP], 0, 2)
-                    quant_w(E, 0, 2)
-                    for h in range(2):
-                        mm_shared(h)
                 quant_tokens(g, woven, T - PIECE, (NEXT_AT, PIECE))
                 quant_tokens(g, middle, PIECE, (0, T - 2 * PIECE))
                 quant_slots(g, slot_stage, 0, (0, S // 2, S))
 
-        def expert(e, raw):
+        def scalar_casts(e, at):
             for a, b in ((0, 2), (2, 4)):
-                load_cast_w(e, raw[:, a * KP : b * KP], a, b)
-            quant_w(e, 0, G)
-            for g in range(G):
-                mm_routed(e, g)
+                load_cast_w(A, 4, e, at + a * QUARTER, a, b)
 
-        def scatter(i, y):
-            a, b = SCATTERS[i]
-            nc.vector.tensor_tensor(window[:].indirect(offsets[:, a // 16 : b // 16]), y, gates[:, a:b], MULT)
-
-        M = G * KP
-        for e in range(2):
-            expert(e, early_w[:, e * M : (e + 1) * M])
-        last = early_w[:, 2 * M - 2 * PIECE : 2 * M].bitcast(BF16)
-        weave(V, F32, 2, last, pairs[G - 1], 0, PIECE)
-        load_cast_w(E, early_w[:, 4 * M + 2 * KP :], 2, 3)
-        quant_w(E, 2, 3)
-        mm_shared(2)
-        quant_tokens(G - 1, last, 0, (0, CUT, PIECE))
-        expert(2, early_w[:, 2 * M : 3 * M])
-        expert(3, early_w[:, 3 * M : 4 * M])
-        y = early_w[:, 4 * M - 2 * C : 4 * M]
-        A(out=y, in_=routed[0][:])
-        scatter(0, y)
-        late_w = place("late_w", 2 * M + KP, F32, pairs_at(0), 256)
-        expert(4, late_w[:, 0:M])
-        y = late_w[:, M - 2 * C : M + 2 * C]
-        A(out=y[:, 0 : 2 * C], in_=routed[1][:])
-        scatter(1, y[:, 0:192])
-        for a, b, at in ((0, 2, M + KP), (2, 3, M), (3, 4, M + 3 * KP)):
-            load_cast_w(5, late_w[:, at : at + (b - a) * KP], a, b)
-            quant_w(5, a, b)
+        def multiply(e, a, b):
+            quant_w(e, a, b)
             for g in range(a, b):
-                mm_routed(5, g)
-            if a == 2:
-                A(out=y[:, 2 * C : 3 * C], in_=routed[2][:])
-                scatter(2, y[:, 192:352])
-        load_cast_w(E, late_w[:, 2 * M :], G - 1, G)
-        quant_w(E, G - 1, G)
-        mm_shared(G - 1)
-        A(out=y[:, 3 * C : 4 * C], in_=routed[3][:])
-        scatter(3, y[:, 352:512])
+                if e == E:
+                    mm_shared(g)
+                else:
+                    mm_routed(e, g)
+
+        def vector_part(e, at, a, b):
+            load_cast_w(V, 2, e, at, a, b)
+            multiply(e, a, b)
+
+        def times_gate(i):
+            a, b = GROUPS[i][0] * C, GROUPS[i][1] * C
+            nc.vector.tensor_tensor(gated[:, a:b], routed[i][:], gates[:, a:b], MULT)
+
+        def scatter(i):
+            a, b = SCATTERS[i]
+            nc.scalar.activation(window[:].indirect(offsets[:, a // 16 : b // 16]), gated[:, a:b], COPY)
+
+        early, late = pairs_at(G), pairs_at(0)
+        for e in range(2):
+            scalar_casts(e, early + e * G * QUARTER)
+            multiply(e, 0, G)
+        last = place("last", 4 * PIECE, BF16, early + 2 * G * QUARTER - 8 * PIECE)
+        weave(V, F32, 2, last, pairs[G - 1], 0, PIECE)
+        quant_tokens(G - 1, last, 0, (0, CUT, PIECE))
+        scalar_casts(2, early + 2 * G * QUARTER)
+        multiply(2, 0, G)
+        scalar_casts(3, early + 3 * G * QUARTER)
+        scalar_casts(4, late)
+        load_cast_w(A, 4, E, early + 4 * G * QUARTER, 0, 1)
+        gated = place("gated", S, F32, late + 2 * QUARTER)
+        ws[3] = place("ws3", G * N, U8, late + 2 * QUARTER + 4 * S)
+        times_gate(0)
+        scatter(0)
+        multiply(3, 0, G)
+        multiply(4, 0, G)
+        multiply(E, 0, 1)
+        times_gate(1)
+        scatter(1)
+        vector_part(5, late + 4 * QUARTER, 0, 2)
+        times_gate(2)
+        scatter(2)
+        vector_part(E, early + 17 * QUARTER, 1, 2)
+        vector_part(5, late + 6 * QUARTER, 2, 4)
+        vector_part(E, early + 18 * QUARTER, 2, 3)
+        times_gate(3)
+        scatter(3)
+        vector_part(E, late + 8 * QUARTER, 3, 4)
 
         a, b = BANKS[0]
         A(out=result[:, a:b], in_=shared[0][:])

@@ -24,11 +24,11 @@ G = K // KP
 H = T // 2
 LOWER, UPPER = (0, H), (H, T)
 HEAD_LOWER, HEAD_UPPER = 416, 960
-BANKS = ((0, 256), (256, 768), (768, 1280))
+BANKS = ((1024, 1280), (512, 1024), (0, 512))
 GROUPS = ((0, 2), (2, 4), (4, 5), (5, 6))
 SCATTERS = ((0, 256), (256, 448), (448, 608), (608, 768))
 PLANE = 8 * T
-PIECE = 576
+PIECE = 640
 CUT = PIECE - 512
 NEXT_AT = PIECE - CUT
 HEAD_SLOTS = S - H
@@ -36,6 +36,7 @@ GATE_RUN = 3
 HEAD_PIECE = 512
 LINK = 64
 QUARTER = 4 * KP
+GATES_AT = 3 * G * PLANE + (5 * G - 1) * QUARTER
 WQUAD_AT = (4096, PLANE, PLANE + 4096, 2 * PLANE, 2 * PLANE + 4096, 3 * PLANE, 0)
 
 
@@ -65,11 +66,12 @@ def tile_moe_shr_lin_none_kernel(tc, xT, w, gate, offs, out):
         slot_scales = keep.tile([P, G * S], U8, name="slot_scales", align_bytes=64)
         token_scales = keep.tile([P, G * T], U8, name="token_scales", align_bytes=64)
         wc = [keep.tile([P, G * N], U32, name=f"wc{e}", align_bytes=64) for e in range(E + 1)]
-        ws = {e: keep.tile([P, G * N], U8, name=f"ws{e}", align_bytes=64) for e in range(E + 1) if e != 3}
+        ws = {e: keep.tile([P, G * N], U8, name=f"ws{e}", align_bytes=64) for e in (0, 1, 2, 4, 5)}
+        shared_ws = {g: keep.tile([P, N], U8, name=f"shared_ws{g}", align_bytes=64) for g in (0, 2, 3)}
         window = keep.tile([P, T], F32, name="window")
         result = keep.tile([P, T], F32, name="result", align_bytes=256)
         gate_cols = keep.tile([P, 2, 8], F32, name="gate_cols")
-        gates = keep.tile([P, S], F32, name="gates")
+        gates = place("gates", S, F32, GATES_AT)
         identity = keep.tile([P, P], F32, name="identity")
         make_identity(nc, identity[:])
         nc.gpsimd.memset(window[:], 0.0)
@@ -136,35 +138,46 @@ def tile_moe_shr_lin_none_kernel(tc, xT, w, gate, offs, out):
         def quant_tokens(g, src, a, cuts):
             quantize(token_codes[g][:, a:T], token_scales[:, g * T + a : (g + 1) * T], src, cuts)
 
+        def wquad(e, a, b):
+            first = G - 1 if e == E and a == G - 1 else 0
+            if (e, first) not in wquads:
+                if first:
+                    wquads[e, first] = place("wquad_last", KP, BF16, GATES_AT)
+                else:
+                    wquads[e, first] = place(f"wquad{e}", G * KP, BF16, WQUAD_AT[e])
+            return wquads[e, first][:, (a - first) * KP : (b - first) * KP]
+
         def load_cast_w(copy, run, e, at, a, b):
             dst = place(f"land{e}{a}", (b - a) * KP, F32, at, 256)[:]
-            if e not in wquads:
-                wquads[e] = place(f"wquad{e}", G * KP, BF16, WQUAD_AT[e])
             src = w[e].rearrange("(g p j) n -> p g (j n)", p=P, j=4)
             dst = dst.rearrange("p (g c) -> p g c", c=KP)
             nc.sync.dma_start(dst, src[:, a:b, :])
             copy(
-                out=wquads[e][:, a * KP : b * KP].rearrange("p (g c i j) -> p g c j i", g=b - a, i=run, j=4),
+                out=wquad(e, a, b).rearrange("p (g c i j) -> p g c j i", g=b - a, i=run, j=4),
                 in_=dst.rearrange("p g (j c i) -> p g c j i", i=run, j=4),
             )
 
+        def w_scales(e, a, b):
+            return shared_ws[a][:] if e == E else ws[e][:, a * N : b * N]
+
         def quant_w(e, a, b):
-            quantize(wc[e], ws[e], wquads[e], (a * N, b * N))
+            quantize(wc[e][:, a * N : b * N], w_scales(e, a, b), wquad(e, a, b), (0, (b - a) * N))
 
         def mm(bank, e, g, codes, scales):
             nc.tensor.matmul_mx(
                 out=bank,
                 lhsT=wc[e][:, g * N : (g + 1) * N].bitcast(FP8X4),
-                lhsT_scale=ws[e][:, g * N : (g + 1) * N],
+                lhsT_scale=w_scales(e, g, g + 1),
                 rhs=codes.bitcast(FP8X4),
                 rhs_scale=scales,
                 start=(g == 0),
                 stop=(g == G - 1),
             )
 
-        def mm_shared(g):
-            for bank, (a, b) in zip(shared, BANKS):
-                mm(bank[:], E, g, token_codes[g][:, a:b], token_scales[:, g * T + a : g * T + b])
+        def mm_shared(g, banks=range(len(BANKS))):
+            for i in banks:
+                a, b = BANKS[i]
+                mm(shared[i][:], E, g, token_codes[g][:, a:b], token_scales[:, g * T + a : g * T + b])
 
         def mm_routed(e, g):
             i = [a <= e < b for a, b in GROUPS].index(True)
@@ -200,13 +213,10 @@ def tile_moe_shr_lin_none_kernel(tc, xT, w, gate, offs, out):
                 quant_slots(g, slot_stage, 0, (0, HEAD_SLOTS))
                 quant_tokens(g, scalar_woven, HEAD_PIECE, (0, HEAD_PIECE, T - HEAD_PIECE))
             else:
-                middle = keep.tile([P, 4 * (T - 2 * PIECE)], BF16, name=f"middle{g}", align_bytes=64)
                 weave(GP, U32, 1, woven, pairs[g], T - PIECE, T)
-                quant_tokens(g, woven, T - PIECE, (0, NEXT_AT))
-                weave(V, F32, 2, middle, pairs[g], PIECE, T - PIECE)
+                quant_tokens(g, woven, T - PIECE, (0, 384))
                 weave(V, F32, 2, slot_stage, gathered[1], 0, S)
-                quant_tokens(g, woven, T - PIECE, (NEXT_AT, PIECE))
-                quant_tokens(g, middle, PIECE, (0, T - 2 * PIECE))
+                quant_tokens(g, woven, T - PIECE, (384, PIECE))
                 quant_slots(g, slot_stage, 0, (0, S // 2, S))
 
         def scalar_casts(e, at):
@@ -239,30 +249,39 @@ def tile_moe_shr_lin_none_kernel(tc, xT, w, gate, offs, out):
             multiply(e, 0, G)
         last = place("last", 4 * PIECE, BF16, early + 2 * G * QUARTER - 8 * PIECE)
         weave(V, F32, 2, last, pairs[G - 1], 0, PIECE)
-        quant_tokens(G - 1, last, 0, (0, CUT, PIECE))
+        quant_tokens(G - 1, last, 0, (512, PIECE))
         scalar_casts(2, early + 2 * G * QUARTER)
         multiply(2, 0, G)
         scalar_casts(3, early + 3 * G * QUARTER)
-        scalar_casts(4, late)
-        load_cast_w(A, 4, E, early + 4 * G * QUARTER, 0, 1)
-        gated = place("gated", S, F32, late + 2 * QUARTER)
-        ws[3] = place("ws3", G * N, U8, late + 2 * QUARTER + 4 * S)
+        load_cast_w(A, 4, 4, late, 0, 2)
+        load_cast_w(A, 4, E, early + 16 * QUARTER, 0, 1)
+        gated = place("gated", S, F32, late)
         times_gate(0)
         scatter(0)
+        load_cast_w(A, 4, E, early + 17 * QUARTER, 1, 2)
+        ws[3] = place("ws3", G * N, U8, late + 4 * S)
         multiply(3, 0, G)
-        multiply(4, 0, G)
         multiply(E, 0, 1)
         times_gate(1)
         scatter(1)
-        vector_part(5, late + 4 * QUARTER, 0, 2)
+        load_cast_w(V, 2, 4, late + 2 * QUARTER, 2, 4)
+        multiply(4, 0, G)
+        shared_ws[1] = place("shared_ws1", N, U8, late + 2 * QUARTER)
+        multiply(E, 1, 2)
+        load_cast_w(V, 2, 5, late + 4 * QUARTER, 0, 2)
         times_gate(2)
         scatter(2)
-        vector_part(E, early + 17 * QUARTER, 1, 2)
+        multiply(5, 0, 2)
         vector_part(5, late + 6 * QUARTER, 2, 4)
         vector_part(E, early + 18 * QUARTER, 2, 3)
         times_gate(3)
         scatter(3)
-        vector_part(E, late + 8 * QUARTER, 3, 4)
+        load_cast_w(V, 2, E, late + 8 * QUARTER, G - 1, G)
+        quant_w(E, G - 1, G)
+        mm_shared(G - 1, (0, 1))
+        last_scales = place("last_scales", 512, U8, GATES_AT)
+        quantize(token_codes[G - 1], last_scales, last, (0, 512))
+        mm(shared[2][:], E, G - 1, token_codes[G - 1][:, 0:512], last_scales[:])
 
         a, b = BANKS[0]
         A(out=result[:, a:b], in_=shared[0][:])
@@ -272,4 +291,4 @@ def tile_moe_shr_lin_none_kernel(tc, xT, w, gate, offs, out):
                 nc.vector.tensor_tensor(result[:, lo:hi], bank[:, lo - a : hi - a], window[:, lo:hi], ADD)
                 nc.sync.dma_start(out[:, lo:hi], result[:, lo:hi])
             if i == 0:
-                nc.sync.dma_start(out[:, 0:a], result[:, 0:a])
+                nc.sync.dma_start(out[:, b:T], result[:, b:T])

@@ -33,9 +33,10 @@ CUT = PIECE - 512
 NEXT_AT = PIECE - CUT
 HEAD_SLOTS = S - H
 GATE_RUN = 3
-HEAD_PIECE = 512
+HEAD_PIECE = 640
 LINK = 64
 QUARTER = 4 * KP
+LAST_AT = 3 * PLANE + 4096
 GATES_AT = 3 * G * PLANE + (5 * G - 1) * QUARTER
 WQUAD_AT = (4096, PLANE, PLANE + 4096, 2 * PLANE, 2 * PLANE + 4096, 3 * PLANE, 0)
 
@@ -142,7 +143,7 @@ def tile_moe_shr_lin_none_kernel(tc, xT, w, gate, offs, out):
             first = G - 1 if e == E and a == G - 1 else 0
             if (e, first) not in wquads:
                 if first:
-                    wquads[e, first] = place("wquad_last", KP, BF16, GATES_AT)
+                    wquads[e, first] = place("wquad_last", KP, BF16, LAST_AT)
                 else:
                     wquads[e, first] = place(f"wquad{e}", G * KP, BF16, WQUAD_AT[e])
             return wquads[e, first][:, (a - first) * KP : (b - first) * KP]
@@ -209,9 +210,9 @@ def tile_moe_shr_lin_none_kernel(tc, xT, w, gate, offs, out):
                 weave(GP, U32, 1, woven, pairs[g], 0, HEAD_PIECE)
                 weave(A, F32, 1, scalar_woven, pairs[g], HEAD_PIECE, T)
                 weave(V, F32, 2, slot_stage, gathered[0], 0, HEAD_SLOTS)
-                quant_tokens(g, woven, 0, (0, HEAD_PIECE))
+                quant_tokens(g, woven, 0, (0, 384, HEAD_PIECE))
                 quant_slots(g, slot_stage, 0, (0, HEAD_SLOTS))
-                quant_tokens(g, scalar_woven, HEAD_PIECE, (0, HEAD_PIECE, T - HEAD_PIECE))
+                quant_tokens(g, scalar_woven, HEAD_PIECE, (0, 384, T - HEAD_PIECE))
             else:
                 weave(GP, U32, 1, woven, pairs[g], T - PIECE, T)
                 quant_tokens(g, woven, T - PIECE, (0, 384))
@@ -247,9 +248,9 @@ def tile_moe_shr_lin_none_kernel(tc, xT, w, gate, offs, out):
         for e in range(2):
             scalar_casts(e, early + e * G * QUARTER)
             multiply(e, 0, G)
-        last = place("last", 4 * PIECE, BF16, early + 2 * G * QUARTER - 8 * PIECE)
-        weave(V, F32, 2, last, pairs[G - 1], 0, PIECE)
-        quant_tokens(G - 1, last, 0, (512, PIECE))
+        rest = place("rest", 4 * CUT, BF16, early + 2 * G * QUARTER - 8 * CUT)
+        weave(V, F32, 2, rest, pairs[G - 1], 512, PIECE)
+        quant_tokens(G - 1, rest, 512, (0, CUT))
         scalar_casts(2, early + 2 * G * QUARTER)
         multiply(2, 0, G)
         scalar_casts(3, early + 3 * G * QUARTER)
@@ -274,14 +275,15 @@ def tile_moe_shr_lin_none_kernel(tc, xT, w, gate, offs, out):
         multiply(5, 0, 2)
         vector_part(5, late + 6 * QUARTER, 2, 4)
         vector_part(E, early + 18 * QUARTER, 2, 3)
+        load_cast_w(A, 4, E, late + 8 * QUARTER, G - 1, G)
         times_gate(3)
         scatter(3)
-        load_cast_w(V, 2, E, late + 8 * QUARTER, G - 1, G)
+        last = place("last", 4 * 512, BF16, GATES_AT)
+        weave(V, F32, 2, last, pairs[G - 1], 0, 512)
         quant_w(E, G - 1, G)
         mm_shared(G - 1, (0, 1))
-        last_scales = place("last_scales", 512, U8, GATES_AT)
-        quantize(token_codes[G - 1], last_scales, last, (0, 512))
-        mm(shared[2][:], E, G - 1, token_codes[G - 1][:, 0:512], last_scales[:])
+        quant_tokens(G - 1, last, 0, (0, 512))
+        mm_shared(G - 1, (2,))
 
         a, b = BANKS[0]
         A(out=result[:, a:b], in_=shared[0][:])

@@ -24,7 +24,7 @@ G = K // KP
 H = T // 2
 LOWER, UPPER = (0, H), (H, T)
 HEAD_LOWER, HEAD_UPPER = 416, 960
-BANKS = ((1024, 1280), (512, 1024), (0, 512))
+BANKS = ((512, 768), (768, 1280), (0, 512))
 GROUPS = ((0, 2), (2, 4), (4, 5), (5, 6))
 SCATTERS = ((0, 256), (256, 448), (448, 608), (608, 768))
 PLANE = 8 * T
@@ -77,8 +77,11 @@ def tile_moe_shr_lin_none_kernel(tc, xT, w, gate, offs, out):
         make_identity(nc, identity[:])
         nc.gpsimd.memset(window[:], 0.0)
 
-        shared = [psum.tile([P, b - a], F32, name=f"shared{a}") for a, b in BANKS]
-        routed = [psum.tile([P, (b - a) * C], F32, name=f"routed{a}") for a, b in GROUPS]
+        def bank(name, cols, i):
+            return psum.tile([P, cols], F32, name=name, offset=i * 2048)
+
+        routed = [bank(f"routed{a}", (b - a) * C, i) for i, (a, b) in enumerate(GROUPS)]
+        shared = [bank(f"shared{a}", b - a, 4 + i) for i, (a, b) in enumerate(BANKS[:2])]
 
         pairs, slot_codes, token_codes, wquads = {}, {}, {}, {}
 
@@ -110,12 +113,13 @@ def tile_moe_shr_lin_none_kernel(tc, xT, w, gate, offs, out):
 
         def spread_gate():
             nc.sync.dma_start(gate_cols[:, :, 0:GATE_RUN], gate[0, :].rearrange("(h p r) -> p h r", h=2, r=GATE_RUN))
-            for h, bank in enumerate(shared[1:]):
+            for h in range(2):
+                turned = bank(f"turned{h}", S // 2, 6 + h)
                 for r in range(GATE_RUN):
-                    nc.tensor.transpose(bank[:, r * P : (r + 1) * P], gate_cols[:, h, r : r + 1].to_broadcast([P, P]), identity[:])
+                    nc.tensor.transpose(turned[:, r * P : (r + 1) * P], gate_cols[:, h, r : r + 1].to_broadcast([P, P]), identity[:])
                 V(
                     out=gates[:, h * S // 2 : (h + 1) * S // 2].rearrange("q (p r) -> q p r", r=GATE_RUN),
-                    in_=bank[:, 0 : S // 2].rearrange("q (r p) -> q p r", r=GATE_RUN),
+                    in_=turned[:].rearrange("q (r p) -> q p r", r=GATE_RUN),
                 )
 
         def gather(g, m):
@@ -164,9 +168,9 @@ def tile_moe_shr_lin_none_kernel(tc, xT, w, gate, offs, out):
         def quant_w(e, a, b):
             quantize(wc[e][:, a * N : b * N], w_scales(e, a, b), wquad(e, a, b), (0, (b - a) * N))
 
-        def mm(bank, e, g, codes, scales):
+        def mm(sums, e, g, codes, scales):
             nc.tensor.matmul_mx(
-                out=bank,
+                out=sums,
                 lhsT=wc[e][:, g * N : (g + 1) * N].bitcast(FP8X4),
                 lhsT_scale=w_scales(e, g, g + 1),
                 rhs=codes.bitcast(FP8X4),
@@ -175,7 +179,7 @@ def tile_moe_shr_lin_none_kernel(tc, xT, w, gate, offs, out):
                 stop=(g == G - 1),
             )
 
-        def mm_shared(g, banks=range(len(BANKS))):
+        def mm_shared(g, banks):
             for i in banks:
                 a, b = BANKS[i]
                 mm(shared[i][:], E, g, token_codes[g][:, a:b], token_scales[:, g * T + a : g * T + b])
@@ -228,7 +232,7 @@ def tile_moe_shr_lin_none_kernel(tc, xT, w, gate, offs, out):
             quant_w(e, a, b)
             for g in range(a, b):
                 if e == E:
-                    mm_shared(g)
+                    mm_shared(g, range(len(shared)))
                 else:
                     mm_routed(e, g)
 
@@ -272,6 +276,9 @@ def tile_moe_shr_lin_none_kernel(tc, xT, w, gate, offs, out):
         load_cast_w(V, 2, 5, late + 4 * QUARTER, 0, 2)
         times_gate(2)
         scatter(2)
+        shared.append(bank("shared0", 512, 2))
+        for g in range(2):
+            mm_shared(g, (2,))
         multiply(5, 0, 2)
         vector_part(5, late + 6 * QUARTER, 2, 4)
         vector_part(E, early + 18 * QUARTER, 2, 3)
@@ -288,9 +295,9 @@ def tile_moe_shr_lin_none_kernel(tc, xT, w, gate, offs, out):
         a, b = BANKS[0]
         A(out=result[:, a:b], in_=shared[0][:])
         nc.gpsimd.tensor_tensor(result[:, a:b], result[:, a:b], window[:, a:b], ADD)
-        for i, (bank, (a, b)) in enumerate(zip(shared[1:], BANKS[1:])):
-            for lo, hi in ((a, (a + b) // 2), ((a + b) // 2, b)):
-                nc.vector.tensor_tensor(result[:, lo:hi], bank[:, lo - a : hi - a], window[:, lo:hi], ADD)
-                nc.sync.dma_start(out[:, lo:hi], result[:, lo:hi])
-            if i == 0:
-                nc.sync.dma_start(out[:, b:T], result[:, b:T])
+        for sums, (a, b) in zip(shared[1:], BANKS[1:]):
+            for lo in (a, a + 256):
+                hi = lo + 256
+                nc.vector.tensor_tensor(result[:, lo:hi], sums[:, lo - a : hi - a], window[:, lo:hi], ADD)
+                end = BANKS[0][1] if hi == BANKS[0][0] else hi
+                nc.sync.dma_start(out[:, lo:end], result[:, lo:end])

@@ -267,10 +267,11 @@ def tile_moe_shr_lin_none_kernel(tc, xT, w, gate, offs, out):
         ws[3] = place("ws3", G * N, U8, late + 4 * S)
         multiply(3, 0, G)
         multiply(E, 0, 1)
+        multiply(4, 0, 2)
         times_gate(1)
         scatter(1)
         load_cast_w(V, 2, 4, late + 2 * QUARTER, 2, 4)
-        multiply(4, 0, G)
+        multiply(4, 2, G)
         shared_ws[1] = place("shared_ws1", N, U8, late + 2 * QUARTER)
         multiply(E, 1, 2)
         load_cast_w(V, 2, 5, late + 4 * QUARTER, 0, 2)

@@ -226,7 +226,7 @@ def tile_moe_shr_lin_none_kernel(tc, xT, w, gate, offs, out):
 
         def scalar_casts(e, at):
             for a, b in ((0, 2), (2, 4)):
-                load_cast_w(A, 4, e, at + a * QUARTER, a, b)
+                load_cast_w(A, 2, e, at + a * QUARTER, a, b)
 
         def multiply(e, a, b):
             quant_w(e, a, b)
@@ -258,12 +258,12 @@ def tile_moe_shr_lin_none_kernel(tc, xT, w, gate, offs, out):
         scalar_casts(2, early + 2 * G * QUARTER)
         multiply(2, 0, G)
         scalar_casts(3, early + 3 * G * QUARTER)
-        load_cast_w(A, 4, 4, late, 0, 2)
-        load_cast_w(A, 4, E, early + 16 * QUARTER, 0, 1)
+        load_cast_w(A, 2, 4, late, 0, 2)
+        load_cast_w(A, 2, E, early + 16 * QUARTER, 0, 1)
         gated = place("gated", S, F32, late)
         times_gate(0)
         scatter(0)
-        load_cast_w(A, 4, E, early + 17 * QUARTER, 1, 2)
+        load_cast_w(A, 2, E, early + 17 * QUARTER, 1, 2)
         ws[3] = place("ws3", G * N, U8, late + 4 * S)
         multiply(3, 0, G)
         multiply(E, 0, 1)
@@ -283,15 +283,16 @@ def tile_moe_shr_lin_none_kernel(tc, xT, w, gate, offs, out):
         multiply(5, 0, 2)
         vector_part(5, late + 6 * QUARTER, 2, 4)
         vector_part(E, early + 18 * QUARTER, 2, 3)
-        load_cast_w(A, 4, E, late + 8 * QUARTER, G - 1, G)
+        load_cast_w(A, 2, E, late + 8 * QUARTER, G - 1, G)
+        last = place("last", 4 * 512, BF16, WQUAD_AT[5])
+        weave(V, F32, 2, last, pairs[G - 1], 0, 512)
         times_gate(3)
         scatter(3)
-        last = place("last", 4 * 512, BF16, GATES_AT)
-        weave(V, F32, 2, last, pairs[G - 1], 0, 512)
         quant_w(E, G - 1, G)
         mm_shared(G - 1, (0, 1))
-        quant_tokens(G - 1, last, 0, (0, 512))
-        mm_shared(G - 1, (2,))
+        last_scales = place("last_scales", 512, U8, GATES_AT)
+        quantize(token_codes[G - 1], last_scales, last, (0, 512))
+        mm(shared[2][:], E, G - 1, token_codes[G - 1][:, 0:512], last_scales[:])
 
         a, b = BANKS[0]
         A(out=result[:, a:b], in_=shared[0][:])

@@ -1,7 +1,6 @@
 from contextlib import ExitStack
 
 import concourse.mybir as mybir
-from concourse.masks import make_identity
 
 K, T, E, C, N = 2048, 1280, 6, 128, 128
 S = E * C
@@ -32,7 +31,6 @@ PIECE = 640
 CUT = PIECE - 512
 NEXT_AT = PIECE - CUT
 HEAD_SLOTS = S - H
-GATE_RUN = 3
 HEAD_PIECE = 640
 LINK = 64
 QUARTER = 4 * KP
@@ -71,10 +69,7 @@ def tile_moe_shr_lin_none_kernel(tc, xT, w, gate, offs, out):
         shared_ws = {g: keep.tile([P, N], U8, name=f"shared_ws{g}", align_bytes=64) for g in (0, 2, 3)}
         window = keep.tile([P, T], F32, name="window")
         result = keep.tile([P, T], F32, name="result", align_bytes=256)
-        gate_cols = keep.tile([P, 2, 8], F32, name="gate_cols")
-        gates = place("gates", S, F32, GATES_AT)
-        identity = keep.tile([P, P], F32, name="identity")
-        make_identity(nc, identity[:])
+        gates = place("gates", S, F32, GATES_AT, 256)
         nc.gpsimd.memset(window[:], 0.0)
 
         def bank(name, cols, i):
@@ -110,17 +105,6 @@ def tile_moe_shr_lin_none_kernel(tc, xT, w, gate, offs, out):
             else:
                 cast_x(A, g, m, raw, *UPPER)
                 cast_x(A, g, m, raw, *LOWER)
-
-        def spread_gate():
-            nc.sync.dma_start(gate_cols[:, :, 0:GATE_RUN], gate[0, :].rearrange("(h p r) -> p h r", h=2, r=GATE_RUN))
-            for h in range(2):
-                turned = bank(f"turned{h}", S // 2, 6 + h)
-                for r in range(GATE_RUN):
-                    nc.tensor.transpose(turned[:, r * P : (r + 1) * P], gate_cols[:, h, r : r + 1].to_broadcast([P, P]), identity[:])
-                V(
-                    out=gates[:, h * S // 2 : (h + 1) * S // 2].rearrange("q (p r) -> q p r", r=GATE_RUN),
-                    in_=turned[:].rearrange("q (r p) -> q p r", r=GATE_RUN),
-                )
 
         def gather(g, m):
             V(gathered[min(g, 1)][:, m, :].bitcast(U32), pairs[g][:, m, :].bitcast(U32).indirect(offsets[:]))
@@ -190,7 +174,6 @@ def tile_moe_shr_lin_none_kernel(tc, xT, w, gate, offs, out):
             a, b = e * C, (e + 1) * C
             mm(routed[i][:, c : c + C], e, g, slot_codes[g][:, a:b], slot_scales[:, g * S + a : g * S + b])
 
-        spread_gate()
         for g in range(G):
             pair_tile = place(f"pairs{g}", 4 * T, BF16, pairs_at(g))
             pairs[g] = pair_tile[:].rearrange("p (m c) -> p m c", m=2)
@@ -257,6 +240,7 @@ def tile_moe_shr_lin_none_kernel(tc, xT, w, gate, offs, out):
         quant_tokens(G - 1, rest, 512, (0, CUT))
         scalar_casts(2, early + 2 * G * QUARTER)
         multiply(2, 0, G)
+        nc.sync.dma_start(gates[:], gate)
         scalar_casts(3, early + 3 * G * QUARTER)
         load_cast_w(A, 2, 4, late, 0, 2)
         load_cast_w(A, 2, E, early + 16 * QUARTER, 0, 1)

from contextlib import ExitStack

import concourse.mybir as mybir

K, T, E, C, N = 2048, 1280, 6, 128, 128
S = E * C

FLOPS = 2 * K * N * (S + T)

F32 = mybir.dt.float32
BF16 = mybir.dt.bfloat16
U32 = mybir.dt.uint32
U16 = mybir.dt.uint16
U8 = mybir.dt.uint8
FP8X4 = mybir.dt.float8_e4m3fn_x4
ADD = mybir.AluOpType.add
MULT = mybir.AluOpType.mult
COPY = mybir.ActivationFunctionType.Copy

P = 128
KP = 512
G = K // KP
H = T // 2
LOWER, UPPER = (0, H), (H, T)
HEAD_LOWER, HEAD_UPPER = 416, 960
BANKS = ((512, 768), (768, 1280), (0, 512))
GROUPS = ((0, 2), (2, 4), (4, 5), (5, 6))
SCATTERS = ((0, 256), (256, 448), (448, 608), (608, 768))
PLANE = 8 * T
PIECE = 640
CUT = PIECE - 512
NEXT_AT = PIECE - CUT
HEAD_SLOTS = S - H
HEAD_PIECE = 640
LINK = 64
QUARTER = 4 * KP
LAST_AT = 3 * PLANE + 4096
GATES_AT = 3 * G * PLANE + (5 * G - 1) * QUARTER
WQUAD_AT = (4096, PLANE, PLANE + 4096, 2 * PLANE, 2 * PLANE + 4096, 3 * PLANE, 0)


def tile_moe_shr_lin_none_kernel(tc, xT, w, gate, offs, out):
    nc = tc.nc
    with ExitStack() as ctx:
        keep = ctx.enter_context(tc.tile_pool(name="keep", bufs=1))
        arena = ctx.enter_context(tc.tile_pool(name="arena", bufs=1))
        psum = ctx.enter_context(tc.psum_pool(name="psum", bufs=1))

        V, A, GP = nc.vector.tensor_copy, nc.scalar.copy, nc.gpsimd.tensor_copy

        def place(name, cols, dtype, at, align=64):
            return arena.tile([P, cols], dtype, name=name, offset=at, align_bytes=align)

        def raw_at(g, m):
            return (g + G * (1 - m)) * PLANE

        def pairs_at(g):
            return (2 * G + g) * PLANE

        offsets = keep.tile([P, S // 16], U16, name="offsets")
        slot_stage = keep.tile([P, 4 * S], BF16, name="slot_stage", align_bytes=64)
        gathered_tiles = [keep.tile([P, 4 * S], BF16, name=f"gathered{i}", align_bytes=64) for i in range(2)]
        gathered = [t[:].rearrange("p (m c) -> p m c", m=2) for t in gathered_tiles]
        scalar_woven = keep.tile([P, 4 * (T - HEAD_PIECE)], BF16, name="scalar_woven", align_bytes=64)
        slot_scales = keep.tile([P, G * S], U8, name="slot_scales", align_bytes=64)
        token_scales = keep.tile([P, G * T], U8, name="token_scales", align_bytes=64)
        wc = [keep.tile([P, G * N], U32, name=f"wc{e}", align_bytes=64) for e in range(E + 1)]
        ws = {e: keep.tile([P, G * N], U8, name=f"ws{e}", align_bytes=64) for e in (0, 1, 2, 4, 5)}
        shared_ws = {g: keep.tile([P, N], U8, name=f"shared_ws{g}", align_bytes=64) for g in (0, 2, 3)}
        window = keep.tile([P, T], F32, name="window")
        result = keep.tile([P, T], F32, name="result", align_bytes=256)
        gates = place("gates", S, F32, GATES_AT, 256)
        nc.gpsimd.memset(window[:], 0.0)

        def bank(name, cols, i):
            return psum.tile([P, cols], F32, name=name, offset=i * 2048)

        routed = [bank(f"routed{a}", (b - a) * C, i) for i, (a, b) in enumerate(GROUPS)]
        shared = [bank(f"shared{a}", b - a, 4 + i) for i, (a, b) in enumerate(BANKS[:2])]

        pairs, slot_codes, token_codes, wquads = {}, {}, {}, {}

        def load_plane(g, m):
            raw = place(f"raw{g}{m}", 2 * T, F32, raw_at(g, m), 256)
            src = xT[g * KP : (g + 1) * KP, :].rearrange("(p m e) t -> p m (e t)", m=2, e=2)[:, m, :]
            nc.sync.dma_start(raw[:, H : 2 * T], src[:, H : 2 * T])
            nc.sync.dma_start(raw[:, 0:H], src[:, 0:H])
            return raw[:].rearrange("p (e t) -> p e t", e=2)

        def cast_x(copy, g, m, raw, a, b):
            copy(
                out=pairs[g][:, m, 2 * a : 2 * b].rearrange("p (c i e) -> p c e i", i=4, e=2),
                in_=raw[:, :, a:b].rearrange("p e (c i) -> p c e i", i=4),
            )

        def bring_plane(g, m):
            raw = load_plane(g, m)
            if g == 0 and m == 1:
                nc.sync.dma_start(offsets[:], offs)
            if g == 0:
                cast_x(V, g, m, raw, H, HEAD_UPPER)
                cast_x(A, g, m, raw, HEAD_UPPER, T)
                cast_x(V, g, m, raw, 0, HEAD_LOWER)
                cast_x(A, g, m, raw, HEAD_LOWER, H)
            else:
                cast_x(A, g, m, raw, *UPPER)
                cast_x(A, g, m, raw, *LOWER)

        def gather(g, m):
            V(gathered[min(g, 1)][:, m, :].bitcast(U32), pairs[g][:, m, :].bitcast(U32).indirect(offsets[:]))

        def weave(copy, dtype, run, dst, src, a, b):
            copy(
                out=dst[:, 0 : 4 * (b - a)].bitcast(dtype).rearrange("p (c i m) -> p c m i", i=run, m=2),
                in_=src[:, :, 2 * a : 2 * b].bitcast(dtype).rearrange("p m (c i) -> p c m i", i=run),
            )

        def quantize(codes, scales, src, cuts):
            for a, b in zip(cuts[:-1], cuts[1:]):
                nc.vector.quantize_mx(
                    out=codes[:, a:b].bitcast(FP8X4), scales=scales[:, a:b], in_=src[:, 4 * a : 4 * b]
                )

        def quant_slots(g, src, a, cuts):
            quantize(slot_codes[g][:, a:S], slot_scales[:, g * S + a : (g + 1) * S], src, cuts)

        def quant_tokens(g, src, a, cuts):
            quantize(token_codes[g][:, a:T], token_scales[:, g * T + a : (g + 1) * T], src, cuts)

        def wquad(e, a, b):
            first = G - 1 if e == E and a == G - 1 else 0
            if (e, first) not in wquads:
                if first:
                    wquads[e, first] = place("wquad_last", KP, BF16, LAST_AT)
                else:
                    wquads[e, first] = place(f"wquad{e}", G * KP, BF16, WQUAD_AT[e])
            return wquads[e, first][:, (a - first) * KP : (b - first) * KP]

        def load_cast_w(copy, run, e, at, a, b):
            dst = place(f"land{e}{a}", (b - a) * KP, F32, at, 256)[:]
            src = w[e].rearrange("(g p j) n -> p g (j n)", p=P, j=4)
            dst = dst.rearrange("p (g c) -> p g c", c=KP)
            nc.sync.dma_start(dst, src[:, a:b, :])
            copy(
                out=wquad(e, a, b).rearrange("p (g c i j) -> p g c j i", g=b - a, i=run, j=4),
                in_=dst.rearrange("p g (j c i) -> p g c j i", i=run, j=4),
            )

        def w_scales(e, a, b):
            return shared_ws[a][:] if e == E else ws[e][:, a * N : b * N]

        def quant_w(e, a, b):
            quantize(wc[e][:, a * N : b * N], w_scales(e, a, b), wquad(e, a, b), (0, (b - a) * N))

        def mm(sums, e, g, codes, scales):
            nc.tensor.matmul_mx(
                out=sums,
                lhsT=wc[e][:, g * N : (g + 1) * N].bitcast(FP8X4),
                lhsT_scale=w_scales(e, g, g + 1),
                rhs=codes.bitcast(FP8X4),
                rhs_scale=scales,
                start=(g == 0),
                stop=(g == G - 1),
            )

        def mm_shared(g, banks):
            for i in banks:
                a, b = BANKS[i]
                mm(shared[i][:], E, g, token_codes[g][:, a:b], token_scales[:, g * T + a : g * T + b])

        def mm_routed(e, g):
            i = [a <= e < b for a, b in GROUPS].index(True)
            c = (e - GROUPS[i][0]) * C
            a, b = e * C, (e + 1) * C
            mm(routed[i][:, c : c + C], e, g, slot_codes[g][:, a:b], slot_scales[:, g * S + a : g * S + b])

        for g in range(G):
            pair_tile = place(f"pairs{g}", 4 * T, BF16, pairs_at(g))
            pairs[g] = pair_tile[:].rearrange("p (m c) -> p m c", m=2)
            bring_plane(g, 1)
            gather(g, 1)
            if g == 0:
                woven = place("woven0", 4 * H, BF16, raw_at(0, 1) + PLANE // 2)
            else:
                woven = place(f"woven{g}", (PLANE + LINK) // 2, BF16, raw_at(g, 1) - LINK)
                if g == 1:
                    weave(GP, U32, 1, woven[:, 4 * NEXT_AT :], gathered[0], HEAD_SLOTS, S)
                    quant_slots(0, woven[:, 4 * NEXT_AT :], HEAD_SLOTS, (0, HEAD_SLOTS, H))
                else:
                    weave(GP, U32, 1, woven[:, 4 * NEXT_AT :], pairs[g - 1], 0, PIECE)
                    quant_tokens(g - 1, woven[:, 4 * NEXT_AT :], 0, (0, CUT, PIECE))
            bring_plane(g, 0)
            token_codes[g] = place(f"token_codes{g}", T, U32, raw_at(g, 0))
            slot_codes[g] = place(f"slot_codes{g}", S, U32, raw_at(g, 0) + PLANE // 2)
            gather(g, 0)
            if g == 0:
                weave(GP, U32, 1, woven, pairs[g], 0, HEAD_PIECE)
                weave(A, F32, 1, scalar_woven, pairs[g], HEAD_PIECE, T)
                weave(V, F32, 2, slot_stage, gathered[0], 0, HEAD_SLOTS)
                quant_tokens(g, woven, 0, (0, 384, HEAD_PIECE))
                quant_slots(g, slot_stage, 0, (0, HEAD_SLOTS))
                quant_tokens(g, scalar_woven, HEAD_PIECE, (0, 384, T - HEAD_PIECE))
            else:
                weave(GP, U32, 1, woven, pairs[g], T - PIECE, T)
                quant_tokens(g, woven, T - PIECE, (0, 384))
                weave(V, F32, 2, slot_stage, gathered[1], 0, S)
                quant_tokens(g, woven, T - PIECE, (384, PIECE))
                quant_slots(g, slot_stage, 0, (0, S // 2, S))

        def scalar_casts(e, at):
            for a, b in ((0, 2), (2, 4)):
                load_cast_w(A, 2, e, at + a * QUARTER, a, b)

        def multiply(e, a, b):
            quant_w(e, a, b)
            for g in range(a, b):
                if e == E:
                    mm_shared(g, range(len(shared)))
                else:
                    mm_routed(e, g)

        def vector_part(e, at, a, b):
            load_cast_w(V, 2, e, at, a, b)
            multiply(e, a, b)

        def times_gate(i):
            a, b = GROUPS[i][0] * C, GROUPS[i][1] * C
            nc.vector.tensor_tensor(gated[:, a:b], routed[i][:], gates[:, a:b], MULT)

        def scatter(i):
            a, b = SCATTERS[i]
            nc.scalar.activation(window[:].indirect(offsets[:, a // 16 : b // 16]), gated[:, a:b], COPY)

        early, late = pairs_at(G), pairs_at(0)
        for e in range(2):
            scalar_casts(e, early + e * G * QUARTER)
            multiply(e, 0, G)
        rest = place("rest", 4 * CUT, BF16, early + 2 * G * QUARTER - 8 * CUT)
        weave(V, F32, 2, rest, pairs[G - 1], 512, PIECE)
        quant_tokens(G - 1, rest, 512, (0, CUT))
        scalar_casts(2, early + 2 * G * QUARTER)
        multiply(2, 0, G)
        nc.sync.dma_start(gates[:], gate)
        scalar_casts(3, early + 3 * G * QUARTER)
        load_cast_w(A, 2, 4, late, 0, 2)
        load_cast_w(A, 2, E, early + 16 * QUARTER, 0, 1)
        gated = place("gated", S, F32, late)
        times_gate(0)
        scatter(0)
        load_cast_w(A, 2, E, early + 17 * QUARTER, 1, 2)
        ws[3] = place("ws3", G * N, U8, late + 4 * S)
        multiply(3, 0, G)
        multiply(E, 0, 1)
        multiply(4, 0, 2)
        times_gate(1)
        scatter(1)
        load_cast_w(V, 2, 4, late + 2 * QUARTER, 2, 4)
        multiply(4, 2, G)
        shared_ws[1] = place("shared_ws1", N, U8, late + 2 * QUARTER)
        multiply(E, 1, 2)
        load_cast_w(V, 2, 5, late + 4 * QUARTER, 0, 2)
        times_gate(2)
        scatter(2)
        shared.append(bank("shared0", 512, 2))
        for g in range(2):
            mm_shared(g, (2,))
        multiply(5, 0, 2)
        vector_part(5, late + 6 * QUARTER, 2, 4)
        vector_part(E, early + 18 * QUARTER, 2, 3)
        load_cast_w(A, 2, E, late + 8 * QUARTER, G - 1, G)
        last = place("last", 4 * 512, BF16, WQUAD_AT[5])
        weave(V, F32, 2, last, pairs[G - 1], 0, 512)
        times_gate(3)
        scatter(3)
        quant_w(E, G - 1, G)
        mm_shared(G - 1, (0, 1))
        last_scales = place("last_scales", 512, U8, GATES_AT)
        quantize(token_codes[G - 1], last_scales, last, (0, 512))
        mm(shared[2][:], E, G - 1, token_codes[G - 1][:, 0:512], last_scales[:])

        a, b = BANKS[0]
        A(out=result[:, a:b], in_=shared[0][:])
        nc.gpsimd.tensor_tensor(result[:, a:b], result[:, a:b], window[:, a:b], ADD)
        for sums, (a, b) in zip(shared[1:], BANKS[1:]):
            for lo in (a, a + 256):
                hi = lo + 256
                nc.vector.tensor_tensor(result[:, lo:hi], sums[:, lo - a : hi - a], window[:, lo:hi], ADD)
                end = BANKS[0][1] if hi == BANKS[0][0] else hi
                nc.sync.dma_start(out[:, lo:end], result[:, lo:end])
